import numpy as np, ml_dtypes
CORES = [1,5,17,21,33,37,49,53]
N = 8
import mx_ref
BF = ml_dtypes.bfloat16
def gentries(a):
    return np.ascontiguousarray(a.reshape(8, 16, -1).transpose(0, 2, 1)).reshape(8, -1)
def gtable(e):
    e = np.asarray(e); return np.ascontiguousarray(e.reshape(8, -1, 16).transpose(0, 2, 1)).reshape(128, -1).astype(np.int32)
def gcols(t, e):
    v = np.concatenate([t.reshape(8, 16, -1, 4), np.zeros((8, 16, 1, 4), BF)], axis=2)
    return np.ascontiguousarray(np.stack([v[g][:, e[g]] for g in range(8)])).reshape(128, -1)
def tile(rs):
    return np.stack(rs, axis=2).reshape(128, -1).astype(BF)
def pick(q, e):
    c = np.concatenate([q[0].reshape(128, -1, 4), np.zeros((128, 1, 4), np.uint8)], axis=1); s = np.concatenate([q[1], np.ones((16, 1), np.uint8)], axis=1)
    return (np.ascontiguousarray(c[:, e].reshape(128, -1)), np.ascontiguousarray(s[:, e]))
def join(*qs):
    return (np.concatenate([q[0] for q in qs], axis=1), np.concatenate([q[1] for q in qs], axis=1))
def put(q, e, v):
    c, s = q[0].reshape(128, -1, 4).copy(), q[1].copy(); c[:, e] = v[0].reshape(128, -1, 4); s[:, e] = v[1]
    return (c.reshape(128, -1), s)
def pk(c, s):
    return (np.ascontiguousarray(c), mx_ref.live(s))
def emit(q):
    return q[0], q[1]
def packed(v, rng):
    q = [mx_ref.quantize(np.ascontiguousarray(v[r])) for r in range(N)]
    return np.stack([a for a, b in q]), np.stack([mx_ref.plane(b, rng) for a, b in q])
def values_of_codes():
    e, c = np.zeros((128, 128, 4), np.float32), np.zeros((128, 2, 4), np.uint8)
    e[np.arange(128), np.arange(128), 0] = 1
    c[:127, :, 0] = np.arange(256).reshape(2, 128).T[:127]
    return mx_ref.matmul(mx_ref.quantize(e.reshape(128, 512).astype(BF)), (c.reshape(128, 8), np.full((16, 2), 127, np.uint8))).T.reshape(-1).astype(np.float64)
CODE_VALUE, SCALE_VALUE = values_of_codes(), 2.0 ** (np.arange(256) - 127.0)
def decode(q):
    return (CODE_VALUE[q[0]].reshape(16, 8, -1, 4) * SCALE_VALUE[q[1]][:, None, :, None] + 0.0).reshape(128, -1).astype(np.float32)
def f(rng, *shape):
    return mx_ref.flush((rng.standard_normal(shape, dtype=np.float32) * np.exp2(rng.integers(-2, 3, shape[:-1] + (1,)))).astype(BF))
def wide(rng, *shape, cols=0):
    v = rng.standard_normal(shape, dtype=np.float32) * np.exp2(rng.integers(-12, 13, shape)).astype(np.float32)
    if cols: v *= np.repeat(np.exp2(rng.integers(-cols, cols + 1, shape[:-2] + (1, shape[-1] // 4))) * (rng.random(shape[:-2] + (1, shape[-1] // 4)) > 0.0625), 4, axis=-1).astype(np.float32)
    return mx_ref.flush(v.astype(BF))
C, K, M, R = 512, 32, 16, 3
BASE = M * np.concatenate([np.arange(K), np.arange(K)])
def matrices(a):
    return a.reshape(8, 16, K // 16, M, M).transpose(0, 2, 1, 3, 4).reshape(8, K, M, M).astype(np.int64)
def stored(m):
    return np.ascontiguousarray(m.reshape(8, K // 16, 16, M, M).transpose(0, 2, 1, 3, 4)).reshape(128, -1)
def numbers_of(rng):
    return {"x": np.array(f(rng, N, 128, 4 * C)), "u": np.array(f(rng, N, 128, 512)), "v": np.array(f(rng, N, 128, 512))}
def nodes(rng):
    return np.stack([gtable(np.stack([rng.permutation(C) for g in range(8)])) for r in range(N)])
def arrows(a):
    a = np.triu(a, 1)
    a = a - a.swapaxes(-1, -2)
    return np.stack([stored(a[r]) for r in range(N)]).astype(np.int32)
def some_arrows(rng):
    return rng.integers(-3, 4, (N, 8, K, M, M)) * (rng.random((N, 8, K, M, M)) < 0.6)
def laid(w, nd):
    w = w.reshape(N, 8, 16, C, 4)
    t = np.zeros_like(w)
    for r in range(N):
        e = gentries(nd[r])
        for g in range(8): t[r, g][:, e[g]] = w[r, g]
    return t.reshape(N, 128, 4 * C).astype(BF)
def weights(rng, still=[], by=1.0):
    w = np.array(f(rng, N, 128, 2048)).reshape(N, 8, 16, 4, 8, 16, 4)
    for i in still:
        w[:, :, i] = 0
        w[:, :, :, :, :, i] = 0
    w = mx_ref.flush((w.astype(np.float32) * np.float32(by)).astype(BF))
    c, s = packed(np.ascontiguousarray(w).reshape(N, 128, 2048), rng)
    return {"wc": c, "ws": s}
def setup_inputs(rng):
    return {**numbers_of(rng), "nd": nodes(rng), "ar": arrows(some_arrows(rng)), **weights(rng)}
def setup_inputs_ties(rng):
    d = numbers_of(rng)
    nd = nodes(rng)
    w = d["x"].reshape(N, 8, 16, C, 4)
    w[:, :, 0] = 0
    w[:, :, 0, :, 0] = rng.integers(1, 4, (N, 8, C)).astype(np.float32).astype(BF)
    u = d["u"].reshape(N, 128, 128, 4)
    u[:, :, ::16] = 0
    o = rng.permutation(N)
    for r in range(N):
        for h in range(0, 128, 16): u[r, h, h, 0] = 0.0 if r == o[0] else -1.0 if r == o[1] else 1.0
    return {"x": laid(w, nd), "u": u.reshape(N, 128, 512), "v": d["v"], "nd": nd, "ar": arrows(some_arrows(rng)), **weights(rng, [0])}
def setup_inputs_near(rng):
    d = numbers_of(rng)
    nd = nodes(rng)
    w = d["x"].astype(np.float32).reshape(N, 8, 16, K, M, 4)
    w[:, :, 0] = 0
    w[:, :, 8:] = 0
    s = rng.integers(0, 16, (N, 8, K, M))
    w[:, :, 8] = ((s[..., None] >> np.arange(4)) & 1) * np.exp2(np.arange(4) - 23.0)
    u = d["u"].reshape(N, 128, 128, 4)
    u[:, :, ::16] = 0
    o = rng.permutation(N) % 4
    for r in range(N):
        k = 1.0 if o[r] == 0 else 2.0 ** -30
        c = rng.choice([-1.0, 1.0], (8, K, 1))
        if o[r] < 2:
            w[r, :, 0, :, :, 0] = c
            w[r, :, 11, :, :, 0] = 2.0 ** -10
        elif o[r] == 2:
            far = np.argsort(rng.random((8, K, M)), axis=2)
            w[r, :, 0, :, :, 0] = 1.0 * (far == 0) - 1.0 * (far == 1)
            for g in rng.permutation(8)[:4]: w[r, g, 0, rng.integers(K), rng.integers(M), 0] = 2.0 ** 26
        else:
            w[r, :, 8] = 0
            w[r, :, 8, :, :, 0] = c * rng.integers(8, 16, (8, K, M)) * 2.0 ** -27
        for h in range(0, 128, 16):
            if o[r] < 2:
                u[r, h, h, 0] = k
                u[r, h + 11, h, 0] = k
            if o[r] == 2: u[r, h, h, 0] = 16.0
            if o[r] < 3: u[r, h + 8, h] = k
            else: u[r, h + 8, h, 0] = k
    return {"x": laid(w, nd), "u": u.reshape(N, 128, 512), "v": d["v"], "nd": nd, "ar": arrows(some_arrows(rng)), **weights(rng, [0, 8, 9, 10, 11, 12, 13, 14, 15])}
def setup_inputs_huge(rng):
    d = numbers_of(rng)
    o = rng.permutation(N)
    a = some_arrows(rng)
    x = 0.8 + 0.1 * rng.random((N, 128, C, 4))
    u = d["u"].reshape(N, 128, 128, 4)
    for r in range(N):
        c = rng.choice([-1.0, 1.0], (C, 1))
        k = 2.0 ** 30 * (1.0 - 0.1 * rng.random((128, 8, 4)))
        if o[r] < 2: c = -np.ones((C, 1))
        if o[r] == 3:
            c = -np.ones((C, 1))
            c[rng.permutation(C)[:K]] = 1.0
            x[r] = 0.9375
            k[:] = 2.0 ** 30
        if o[r] % 2 == 1: a[r] = 0
        x[r] *= c * (2.0 ** 30 if o[r] % 2 == 1 else 2.0 ** 28 if o[r] == 0 else 2.0 ** 27)
        u[r, :, ::16] = k.astype(np.float32).astype(BF)
    return {"x": x.astype(np.float32).reshape(N, 128, 4 * C).astype(BF), "u": u.reshape(N, 128, 512), "v": d["v"], "nd": nodes(rng), "ar": arrows(a), **weights(rng, [], 2.0 ** -14)}
def setup_inputs_knots(rng):
    d = numbers_of(rng)
    e = rng.permutation(N)
    kind = rng.integers(0, 4, (N, 8, K, 1, 1))
    kind[e[0]] = 0
    kind[e[1]] = 1
    sign = rng.choice([-1, 1], (N, 8, K, M, M))
    half = sign * (rng.random((N, 8, K, M, M)) < 0.5)
    a = np.where(kind == 0, 0, np.where(kind == 1, sign * rng.integers(1, 4, (N, 8, K, M, M)), np.where(kind == 2, half, 3 * half)))
    place = np.arange(8)[:, None, None] * 4 + np.arange(4)
    most = place == rng.integers(0, 32, (N, 16, 1, C, 1))
    x = (129.0 + 2.0 * rng.integers(0, 64, (N, 16, 8, C, 4))) * np.exp2(-7.0 - rng.integers(8, 15, (N, 16, 8, C, 4)))
    x = np.where(most, 1.96875, x) * rng.choice([-1.0, 1.0], (N, 16, 8, C, 4)) * np.exp2(rng.integers(-2, 3, (N, 16, 1, C, 1)))
    return {"x": x.astype(np.float32).reshape(N, 128, 4 * C).astype(BF), "u": d["u"], "v": d["v"], "nd": nodes(rng), "ar": arrows(a), **weights(rng)}
def setup_inputs_spread(rng):
    d = setup_inputs(rng)
    d["x"] = wide(rng, N, 128, 4 * C, cols=6)
    return d
def check_inputs(d):
    b = []
    for k in ("x", "u", "v"):
        a = np.abs(d[k].astype(np.float32))
        if not (np.isfinite(a).all() and ((a == 0) | (a >= 2.0 ** -30) & (a <= 2.0 ** 30)).all()): b.append("a value of " + k)
    none, least, most = [emit(mx_ref.quantize(np.full((128, 16), k, np.float32).astype(BF)))[1][0, 0] for k in (0.0, 2.0 ** -30, 2.0 ** 30)]
    for r in range(N):
        if (np.sort(gentries(d["nd"][r]), axis=1) != np.arange(C)).any(): b.append("nd: a group without every column once")
        a = matrices(d["ar"][r])
        if (np.abs(a) > 3).any(): b.append("an entry of ar")
        if (a != -a.swapaxes(-1, -2)).any(): b.append("ar: B[j, i] isn't -B[i, j]")
        if ((d["wc"][r] & 0x7F) == 0x7F).any(): b.append("wc: a code that is no number")
        s = mx_ref.live(d["ws"][r])
        if ((s != none) & ((s < least) | (s > most))).any(): b.append("ws: a scale out of range")
    return b
def parts(t, n, e):
    return gcols(t, np.where(e < 0, -1, np.take_along_axis(n, BASE + np.maximum(e, 0), axis=1))).astype(np.float32)
def pair(t, n, w):
    e = np.argsort(-w, axis=2, kind="stable")[:, :, :2]
    e = np.where(np.take_along_axis(w, e, axis=2) > 0, e, -1)
    return ((parts(t, n, e[:, :, 0]) + parts(t, n, e[:, :, 1])) * np.float32(0.5)).astype(BF).astype(np.float32)
def reference(x, u, v, nd, ar, wc, ws):
    qu = [mx_ref.quantize(u[r]) for r in range(N)]
    lay = [pk(wc[r], ws[r]) for r in range(N)]
    now = [x[r] for r in range(N)]
    node = [gentries(nd[r]) for r in range(N)]
    arrow = [matrices(ar[r]) for r in range(N)]
    for t in range(R):
        held, made, sent, into = [], [], [], []
        for r in range(N):
            q = mx_ref.quantize(now[r])
            own = decode(q).astype(BF)
            s = mx_ref.matmul(qu[r], q)[::16] + np.float32(0.0)
            s = np.take_along_axis(s, node[r], axis=1).reshape(8, K, M)
            first = np.argmax(s, axis=2)
            row = np.take_along_axis(arrow[r], first[:, :, None, None], axis=2)[:, :, 0]
            free = (row == 0) & (np.arange(M) != first[:, :, None])
            second = np.argmax(np.where(free, s, -np.inf), axis=2)
            k = np.concatenate([first, second], axis=1)
            full = np.concatenate([np.ones((8, K), bool), free.any(axis=2)], axis=1)
            row = np.concatenate([row, np.take_along_axis(arrow[r], second[:, :, None, None], axis=2)[:, :, 0]], axis=1) * full[:, :, None]
            y = (np.maximum(pair(own, node[r], -row), pair(own, node[r], row)) - parts(own, node[r], np.where(full, k, -1))).astype(BF)
            held.append(own)
            made.append(y)
            sent.append(mx_ref.quantize(y))
            e = np.tile(np.arange(C), (8, 1))
            g, i = np.nonzero(full)
            e[g, np.take_along_axis(node[r], BASE + k, axis=1)[g, i]] = C + i
            into.append(e)
            more = (np.abs(row)[:, :, :, None] * row[:, :, None, :] - row[:, :, :, None] * np.abs(row)[:, :, None, :]) // 2
            turn = np.ones((8, 2 * K, M), np.int64)
            np.put_along_axis(turn, k[:, :, None], np.where(full, -1, 1)[:, :, None], axis=2)
            turn = turn[:, :K] * turn[:, K:]
            arrow[r] = np.clip(arrow[r] + more[:, :K] + more[:, K:], -3, 3) * turn[:, :, :, None] * turn[:, :, None, :]
        for r in range(N):
            q = sent[(r - 1) % N]
            new = tile([mx_ref.matmul(pick(lay[r], np.arange(128 * b, 128 * b + 128)), q) * np.float32(0.03125) + made[r][:, b::4].astype(np.float32) for b in range(4)])
            now[r] = gcols(np.concatenate([held[r], new], axis=1), into[r])
    y, oa = np.zeros((N, 128, C), np.float32), np.zeros(ar.shape, np.float32)
    oc, osc = np.zeros((N, 128, 4 * C), np.uint8), np.zeros((N, 16, C), np.uint8)
    for r in range(N):
        q = mx_ref.quantize(now[r])
        y[r] = mx_ref.matmul(mx_ref.quantize(v[r]), q)
        oa[r] = stored(arrow[r])
        oc[r], osc[r] = emit(q)
    return {"y": y, "oa": oa, "oc": oc, "osc": osc}

@@ -1,0 +1,456 @@
+from concourse.bass import DstId, RemoteDMATransfer
+from concourse.mybir import dt, AluOpType, AxisListType, ActivationFunctionType
+
+OP = AluOpType
+AF = ActivationFunctionType
+R = 3
+W = 2176
+ROW, BLK = 17, 323
+UNIT = 131072.0
+BIG = 1.0e29
+
+CODES, PLANE, BF, F32, I32, U16 = "float8_e4m3fn_x4", "uint8", "bfloat16", "float32", "int32", "uint16"
+SCRATCH = {"PS": ("psum", [128, 3072], F32)}
+for _n, _w, _d in (
+    ("XT", 2048, BF), ("UT", 512, BF), ("VT", 512, BF), ("ET", 528, BF), ("ZT", 512, BF),
+    ("UQ", 128, CODES), ("US", 128, PLANE), ("UQR", 128, CODES), ("USR", 128, PLANE), ("VQ", 128, CODES), ("VS", 128, PLANE),
+    ("WQ", 512, CODES), ("WS", 512, PLANE), ("EQ", 512, CODES), ("ES", 512, PLANE), ("ZQ", 128, CODES), ("ZS", 128, PLANE),
+    ("NDI", 32, I32), ("ARI", 512, I32), ("IA", 360, I32), ("FA", 400, F32),
+    ("ONE", 592, BF), ("IOT", 512, F32), ("KI", 512, F32), ("OWN", 512, F32),
+    ("L32", 32, U16), ("UL", 8, U16), ("SL", 36, U16), ("AL", 38, U16), ("OUTL", 38, U16), ("OL", 32, U16),
+    ("G0", 512, F32), ("G1", 256, F32), ("G2", 128, F32), ("G3", 64, F32), ("N4", 32, F32), ("HL", 80, F32),
+    ("CM", 512, F32), ("PW", 528, F32), ("FOLD", 544, BF), ("YC", 323, BF), ("KEEP", 578, BF), ("RS0", 34, F32), ("RST", 34, F32),
+    ("SEG", 152, F32), ("PRI", 152, F32), ("CC", 152, F32), ("ZK", 8, F32), ("ARB", 528, BF),
+    ("SG", 544, F32), ("Z", 544, F32), ("RX", 34, F32), ("TT", 34, F32), ("IX", 4, F32), ("KAP", 646, BF), ("DM", 646, BF),
+    ("RSF", 646, BF), ("RSS", 646, BF), ("GT", 34, F32), ("S2", 34, F32), ("KEY", 152, F32), ("RK", 156, F32), ("SK", 152, F32),
+    ("DEC", 16, I32), ("DCM", 16, I32), ("LL", 64, U16), ("KC", 4, F32), ("KL", 16, U16),
+    ("KF", 256, BF), ("AB", 512, BF), ("IO2", 512, BF), ("M2", 256, BF), ("MH", 256, BF), ("YT", 512, BF), ("YW", 256, BF),
+    ("V32", 256, BF), ("VV", 256, BF), ("CLN", 68, BF), ("RVF", 48, BF), ("RVS", 48, BF), ("FV", 48, BF), ("FG", 68, BF),
+    ("FS", 68, BF), ("FH", 34, BF), ("SPF", 578, BF), ("SPS", 578, BF), ("SPA", 578, BF), ("SPX", 578, BF),
+    ("D0F", 1776, BF), ("D0S", 1776, BF), ("D0X", 1776, BF), ("TA", 1784, BF), ("TB", 1744, BF), ("TC", 1744, BF), ("TD", 1744, BF),
+    ("OAO", 512, F32), ("YO", 512, F32),
+) + tuple(("F%d" % t, W, BF) for t in range(R)) + tuple((n + "%d" % t, 128, d) for t in range(R) for n, d in (("SQ", CODES), ("SS", PLANE), ("LQ", CODES), ("LS", PLANE))) \
+  + tuple((n + "%d" % t, 512, d) for t in range(R + 1) for n, d in (("XQ", CODES), ("XS", PLANE))):
+    SCRATCH[_n] = ("sbuf", [128, _w], _d)
+
+SEMAPHORES = ["cv", "cs", "ct", "cp", "left"] + ["arr%d" % t for t in range(R)] + ["dm%d" % i for i in range(40)]
+COUNTER = {"v": "cv", "s": "cs", "t": "ct", "p": "cp"}
+PART = {n: ("IA", a, w) for n, a, w in (("PI", 0, 1), ("PMI", 8, 1), ("ULI", 16, 8), ("EI", 24, 38), ("EE", 64, 38), ("EM", 104, 38), ("QD", 144, 38),
+                                       ("OLI", 184, 32), ("OLX", 216, 32), ("NI", 248, 32), ("NHI", 280, 32), ("NLO", 312, 32))}
+PART.update({n: ("FA", a, w) for n, a, w in (("PM", 0, 1), ("H17", 8, 38), ("H256", 48, 38), ("YE", 88, 38), ("XE", 128, 38), ("T1", 168, 38),
+                                            ("T2", 208, 38), ("T3", 248, 38), ("T4", 288, 38), ("T5", 328, 38))})
+
+
+def make_tracker(g, T):
+    eng = {"v": g.vector, "s": g.scalar, "t": g.tensor, "p": g, "y": g.sync}
+    count = {}
+    known = {q: {} for q in eng}
+    hist = {}
+
+    def view(name, lo=0, hi=None, step=1, ind=None, cast=None):
+        if name in PART:
+            name, at, width = PART[name]
+            lo, hi = lo + at, (width if hi is None else hi) + at
+        t = T[name]
+        hi = int(t.shape[1]) if hi is None else hi
+        ap = t[:, lo:hi:step] if step != 1 else t[:, lo:hi]
+        deps = [(name, lo, hi)]
+        if cast is not None:
+            ap = ap.bitcast(cast)
+        if ind is not None:
+            ap = ap.indirect(T[ind[0]][:, ind[1]:ind[2]])
+            deps.append(ind)
+        return ap, deps
+
+    def wait(q, sem, val):
+        if known[q].get(sem, 0) < val:
+            known[q][sem] = val
+            eng[q].wait_ge(T.sem[sem], val)
+
+    def before(q, reads, writes):
+        need = {}
+        for acc, wr in ((reads, False), (writes, True)):
+            for name, lo, hi in acc:
+                for (a, b, w, sem, val, oq) in hist.get(name, []):
+                    if a < hi and lo < b and (w or wr):
+                        need[sem] = max(need.get(sem, 0), val)
+        for sem in need:
+            wait(q, sem, need[sem])
+
+    def after(q, reads, writes, sem, val):
+        for name, lo, hi in writes:
+            keep = [h for h in hist.get(name, []) if not (lo <= h[0] and h[1] <= hi)]
+            hist[name] = keep + [(lo, hi, True, sem, val, q)]
+        for name, lo, hi in reads:
+            keep = [h for h in hist.get(name, []) if h[2] or h[5] != q or not (lo <= h[0] and h[1] <= hi)]
+            hist[name] = keep + [(lo, hi, False, sem, val, q)]
+
+    def bank(d):
+        return (d[0], d[1] // 512 * 512, (d[2] + 511) // 512 * 512) if d[0] == "PS" else d
+
+    def call(q, fn, outs, ins):
+        reads = [d for v in ins for d in v[1] if d[0] != "PS"] + [d for v in outs for d in v[1][1:]]
+        writes = [bank(v[1][0]) for v in outs] + [bank(d) for v in ins for d in v[1] if d[0] == "PS"]
+        before(q, reads, writes)
+        sem = COUNTER[q]
+        count[sem] = count.get(sem, 0) + 1
+        fn(eng[q]).then_inc(T.sem[sem], 1)
+        after(q, reads, writes, sem, count[sem])
+
+    def dma(q, out, in_):
+        before(q, in_[1], out[1])
+        n = count.get("dma", 0)
+        count["dma"] = n + 1
+        eng[q].dma_start(out[0], in_[0]).then_inc(T.sem["dm%d" % n], 16)
+        after("dma%d" % n, in_[1], out[1], "dm%d" % n, 16)
+        count["dm%d" % n] = 16
+
+    return view, wait, before, after, call, dma, count
+
+
+def rank_program(g, core, T, topo):
+    rank = T.rank_of(core)
+    if rank is None:
+        return
+    f, wait, before, after, call, dma, count = make_tracker(g, T)
+
+    def tt(out, a, b, op):
+        call("v", lambda e: e.tensor_tensor(out[0], a[0], b[0], op), [out], [a, b])
+
+    def ts(out, a, s1, op0, s2=None, op1=None):
+        ins = [a] + [s for s in (s1, s2) if isinstance(s, tuple)]
+        x1 = s1[0] if isinstance(s1, tuple) else s1
+        x2 = s2[0] if isinstance(s2, tuple) else s2
+        if op1 is None:
+            call("v", lambda e: e.tensor_scalar(out[0], a[0], x1, None, op0), [out], ins)
+        else:
+            call("v", lambda e: e.tensor_scalar(out[0], a[0], x1, x2, op0, op1), [out], ins)
+
+    def cp(out, a):
+        call("v", lambda e: e.tensor_copy(out[0], a[0]), [out], [a])
+
+    def fill(out, c):
+        call("v", lambda e: e.memset(out[0], c), [out], [])
+
+    def scan(out, d0, d1, init, op0, op1):
+        call("v", lambda e: e.tensor_tensor_scan(out[0], d0[0], d1[0], init, op0, op1), [out], [d0, d1])
+
+    def total(out, a):
+        call("v", lambda e: e.tensor_reduce(out[0], a[0], AxisListType.X, OP.add), [out], [a])
+
+    def quant(qn, sn, lo, hi, a):
+        q, s = f(qn, lo, hi), f(sn, lo, hi)
+        call("v", lambda e: e.quantize_mx(q[0], s[0], a[0]), [q, s], [a])
+
+    def act(out, a, func=AF.Copy, scale=1.0, bias=None):
+        if bias is None:
+            call("s", lambda e: e.activation(out[0], a[0], func, scale=scale), [out], [a])
+        elif isinstance(bias, tuple):
+            call("s", lambda e: e.activation(out[0], a[0], func, bias=bias[0], scale=scale), [out], [a, bias])
+        else:
+            call("s", lambda e: e.activation(out[0], a[0], func, bias=bias, scale=scale), [out], [a])
+
+    def mm(out, l, ls, r, rs):
+        call("t", lambda e: e.matmul_mx(out[0], l[0], ls[0], r[0], rs[0], True, True), [out], [l, ls, r, rs])
+
+    def iota(out, pattern, base=0, cm=0, small=True):
+        if small:
+            call("p", lambda e: e.iota(out[0], pattern, base, cm, allow_small_or_imprecise_dtypes=True), [out], [])
+        else:
+            call("p", lambda e: e.iota(out[0], pattern, base, cm), [out], [])
+
+    def affine(out, a, pattern, op, fillv, base, cm):
+        call("p", lambda e: e.affine_select(out[0], a[0], pattern, op, fillv, base, cm), [out], [a])
+
+    def zeros(out, n):
+        iota(out, [[0, n]])
+
+    dma("y", f("NDI"), (T.nd[:, :], []))
+    dma("s", f("UT"), (T.u[:, :], []))
+    dma("y", f("XT", 0, 1024), (T.x[:, 0:1024], []))
+    dma("s", f("XT", 1024, 2048), (T.x[:, 1024:2048], []))
+    dma("y", f("ARI"), (T.ar[:, :], []))
+    dma("s", f("WQ", cast=dt.uint8), (T.wc[:, :], []))
+    dma("y", f("WS"), (T.ws[:, :], []))
+    dma("s", f("VT"), (T.v[:, :], []))
+
+    fill(f("ONE"), 1.0)
+    fill(f("RS0"), BIG)
+    iota(f("PI"), [[0, 1]], 0, 1, small=False)
+    iota(f("EI"), [[16, 38]], small=False)
+    iota(f("KI"), [[1, 16], [0, 32]])
+    iota(f("IOT"), [[4, 512]])
+    iota(f("ULI"), [[16, 8]], small=False)
+    affine(f("FOLD"), f("ONE", 0, 544), [[0, 34], [1, 16]], OP.not_equal, 0.0, 0, 0)
+    affine(f("RST"), f("RS0"), [[0, 2], [1, 17]], OP.not_equal, -BIG, 0, 0)
+    affine(f("ET"), f("ONE", 0, 528), [[-1, 528]], OP.is_equal, 0.0, 3, 4)
+    zeros(f("TA", 1734, 1784), 50)
+    iota(f("YC"), [[0, 19], [1, 17]])
+    iota(f("SEG"), [[1, 8], [0, 19]], 1)
+    iota(f("PRI"), [[0, 8], [-4096, 19]], 65536)
+    zeros(f("F0", 2048, W), 128)
+    zeros(f("YT", 256, 512), 256)
+    affine(f("KEEP"), f("ONE", 0, 578), [[0, 34], [1, 17]], OP.not_equal, 0.0, 0, 0)
+    zeros(f("SPF"), 578)
+    zeros(f("D0F", 0, 1776, 3), 592)
+    zeros(f("SPS"), 578)
+    zeros(f("SPA"), 578)
+    zeros(f("D0S", 0, 1776, 3), 592)
+    zeros(f("SPX"), 578)
+    zeros(f("D0X", 0, 1776, 3), 592)
+    zeros(f("ZT"), 512)
+    for j in (1, 2):
+        zeros(f("TD", j, 1734, 3), 578)
+    for t in range(1, R):
+        zeros(f("F%d" % t, 2048, W), 128)
+    iota(f("OLI"), [[867, 2], [51, 16]], 56, small=False)
+    iota(f("OLX"), [[0, 2], [1, 16]], small=False)
+
+    ts(f("PMI"), f("PI"), 15, OP.bitwise_and)
+    cp(f("PM"), f("PMI"))
+    pm = f("PM")
+    ts(f("EE"), f("EI"), pm, OP.add)
+    ts(f("EM"), f("EE"), 3856.0, OP.mult)
+    ts(f("QD"), f("EM"), 16, OP.logical_shift_right)
+    ts(f("H17"), f("QD"), 17.0, OP.is_ge, 17.0, OP.mult)
+    ts(f("T1"), f("QD"), -17.0, OP.mult)
+    tt(f("XE"), f("QD"), f("H17"), OP.subtract)
+    tt(f("YE"), f("T1"), f("EE"), OP.add)
+    ts(f("OWN"), f("KI"), pm, OP.is_equal)
+    for h in range(2):
+        cp(f("L32", h, 32, 2), f("NDI", 16 * h, 16 * h + 16))
+    cp(f("UL"), f("ULI"))
+    tt(f("G0"), f("IOT", ind=("L32", 0, 32)), f("OWN"), OP.mult)
+    quant("UQ", "US", 0, 128, f("UT"))
+    cp(f("UQR", cast=dt.uint32), f("UQ", cast=dt.uint32, ind=("UL", 0, 8)))
+    cp(f("USR"), f("US", ind=("UL", 0, 8)))
+    tt(f("G1"), f("G0", 0, 256), f("G0", 256, 512), OP.add)
+    tt(f("G2"), f("G1", 0, 128), f("G1", 128, 256), OP.add)
+    tt(f("G3"), f("G2", 0, 64), f("G2", 64, 128), OP.add)
+    tt(f("N4"), f("G3", 0, 32), f("G3", 32, 64), OP.add)
+    cp(f("CM", ind=("L32", 0, 32)), f("OWN"))
+    fill(f("SL"), 512)
+    for h in range(2):
+        ts(f("SL", 18 * h + 1, 18 * h + 17), f("N4", 16 * h, 16 * h + 16), 0.25, OP.mult)
+    fill(f("PW", 512, 528), -BIG / 32)
+
+    def scores(t, src):
+        for a in range(2):
+            quant("XQ%d" % t, "XS%d" % t, 256 * a, 256 * a + 256, f(src, 1024 * a, 1024 * a + 1024))
+            mm(f("PS", 512 * a, 512 * a + 256), f("UQR"), f("USR"), f("XQ%d" % t, 256 * a, 256 * a + 256), f("XS%d" % t, 256 * a, 256 * a + 256))
+        for a in range(2):
+            tt(f("PW", 256 * a, 256 * a + 256), f("PS", 512 * a, 512 * a + 256), f("CM", 256 * a, 256 * a + 256), OP.mult)
+        act(f("SG", 0, 272), f("PW", 0, 528, ind=("SL", 0, 17)))
+        act(f("SG", 272, 544), f("PW", 0, 528, ind=("SL", 18, 35)))
+
+    def unpack(t):
+        for b in range(4):
+            mm(f("PS", 1024 + 512 * b, 1536 + 512 * b), f("EQ", 128 * b, 128 * b + 128), f("ES", 128 * b, 128 * b + 128), f("XQ%d" % t), f("XS%d" % t))
+        for b in range(4):
+            act(f("F%d" % t, b, 2048, 4), f("PS", 1024 + 512 * b, 1536 + 512 * b))
+
+    def differences():
+        for h in range(2):
+            tt(f("DM", BLK * h, BLK * h + 289), f("TA", 867 * h + 2, 867 * h + 867, 3), f("TA", 867 * h + 5, 867 * h + 870, 3), OP.subtract)
+
+    scores(0, "XT")
+
+    ts(f("ARB", 0, 512), f("ARI"), -UNIT, OP.mult)
+    fill(f("ARB", 512, 520), 0.0)
+    fill(f("ARB", 520, 528), UNIT / 64)
+    ts(f("H256"), f("QD"), 17.0, OP.is_ge, 256.0, OP.mult)
+    ts(f("T1"), f("XE"), 0.0, OP.is_equal, 1000.0, OP.mult)
+    ts(f("T3"), f("YE"), 0.0, OP.is_equal, 1000.0, OP.mult)
+    ts(f("T2"), f("XE"), 16.0, OP.mult, -17.0, OP.add)
+    tt(f("T4"), f("XE"), f("T1"), OP.add)
+    tt(f("T5"), f("T1"), f("T3"), OP.add)
+    tt(f("T1"), f("T2"), f("YE"), OP.add)
+    tt(f("T3"), f("H256"), f("T5"), OP.add)
+    tt(f("T2"), f("T4"), f("YE"), OP.is_equal)
+    tt(f("T5"), f("T1"), f("T3"), OP.add)
+    ts(f("T4"), f("T2"), 520.0, OP.mult)
+    ts(f("T1"), f("T5"), 512.0, OP.min)
+    tt(f("T3"), f("T1"), f("T4"), OP.max)
+    cp(f("AL"), f("T3"))
+    act(f("TA", 2, 1778, 3), f("ARB", ind=("AL", 0, 37)))
+    for b in range(4):
+        quant("EQ", "ES", 128 * b, 128 * b + 128, f("ET", 3 - b, 515 - b))
+    unpack(0)
+    cp(f("NI"), f("N4"))
+    ts(f("NHI"), f("NI"), 1920, OP.bitwise_and)
+    ts(f("NLO"), f("NI"), 127, OP.bitwise_and)
+    fill(f("HL"), 0.0)
+    for h in range(2):
+        fill(f("HL", 36 * h, 36 * h + 1), 2048.0)
+        ts(f("HL", 36 * h + 18, 36 * h + 19), pm, 4.0, OP.mult, 64.0 * h, OP.add)
+        cp(f("HL", 36 * h + 1, 36 * h + 17), f("NHI", 16 * h, 16 * h + 16))
+        cp(f("HL", 36 * h + 19, 36 * h + 35), f("NLO", 16 * h, 16 * h + 16))
+    for h in range(2):
+        for j in range(2):
+            tt(f("DM", BLK * h + 289 + 17 * j, BLK * h + 306 + 17 * j), f("HL", 36 * h + 18 * j, 36 * h + 18 * j + 17), f("HL", 36 * h + 18 * j + 1, 36 * h + 18 * j + 18), OP.subtract)
+    differences()
+
+    def late_constants():
+        ts(f("ZK"), f("SEG", 0, 152, 19), 1048576.0, OP.mult, 71680.0, OP.add)
+        ts(f("CC"), f("SEG"), 1048576.0, OP.mult)
+        tt(f("CC"), f("CC"), f("PRI"), OP.add)
+        for s in range(8):
+            a = 19 * s + 1
+            tt(f("CC", a, a + 16), f("CC", a, a + 16), f("N4", 16 * (s % 2), 16 * (s % 2) + 16), OP.add)
+        fill(f("RK", 0, 1), -BIG)
+
+    def more_constants():
+        tt(f("T2"), f("YE"), f("H17"), OP.add)
+        cp(f("OUTL"), f("T2"))
+        quant("ZQ", "ZS", 0, 128, f("ZT"))
+        for t in range(R):
+            dma("y", f("LQ%d" % t, 64, 128, cast=dt.uint8), f("ZQ", 64, 128, cast=dt.uint8))
+            dma("y", f("LS%d" % t, 64, 128), f("ZS", 64, 128))
+
+    def choose(s, ix, out):
+        scan(f("RX"), f("RST"), s, 0.0, OP.min, OP.max)
+        for h in range(2):
+            ts(f("TT", ROW * h, ROW * h + ROW), f("RX", ROW * h, ROW * h + ROW), f("RX", ROW * h + 16, ROW * h + 17), OP.is_lt)
+        for h in range(2):
+            total(f("IX", ix + h, ix + h + 1), f("TT", ROW * h, ROW * h + ROW))
+        for h in range(2):
+            ts(f("KAP", BLK * h, BLK * h + BLK), f("YC"), f("IX", ix + h, ix + h + 1), OP.is_gt)
+        scan(f(out), f("KAP"), f("DM"), 0.0, OP.mult, OP.add)
+
+    def keys(j, rs):
+        r = f(rs, 16, 646, 17)
+        for io in range(2):
+            a = 76 * io + 38 * j
+            tt(f("KEY", a, a + 38), f("CC", a, a + 38), r, OP.add if io else OP.subtract)
+
+    def column(j, rs):
+        tt(f("KC", 2 * j, 2 * j + 2), f(rs, 305, 646, BLK), f(rs, 322, 646, BLK), OP.add)
+
+    nxt = T.cores[(rank + 1) % len(T.cores)]
+    rid, pid, _ = topo.addr(nxt)
+    mask = sum(1 << e for e in topo.engines(core, nxt)[:8])
+    engines = 8
+
+    def send(t):
+        q, s = f("SQ%d" % t, 0, 64, cast=dt.uint8), f("SS%d" % t, 0, 64)
+        before("p", q[1] + s[1], [])
+        g.remote_dma(T["LQ%d" % t][:, 0:64].bitcast(dt.uint8), q[0], T.sem["arr%d" % t], T.sem["left"], pid, rid, mask)
+        g.remote_dma(T["LS%d" % t][:, 0:64], s[0], T.sem["arr%d" % t], T.sem["left"], pid, rid, mask)
+        after("in%d" % t, [], [("LQ%d" % t, 0, 64), ("LS%d" % t, 0, 64)], "arr%d" % t, 2 * engines)
+        count["arr%d" % t] = 2 * engines
+        count["left"] = count.get("left", 0) + 2 * engines
+
+    def clean(j, rs, rv, sp):
+        for h in range(2):
+            act(f("CLN", 34 * j + ROW * h, 34 * j + ROW * h + ROW), f(rs, BLK * h + 16, BLK * h + 289, 17), AF.Identity, 1.0 / UNIT, 192.0)
+        act(f(rv, 0, 34), f("CLN", 34 * j, 34 * j + 34), AF.Identity, UNIT, -192.0 * UNIT)
+        act(f(sp, 0, 578, 17), f("CLN", 34 * j, 34 * j + 34), AF.Identity, UNIT, -192.0 * UNIT)
+
+    def rows(sp, out, lo):
+        scan(f(out, lo, 1734, 3), f("KEEP"), f(sp), 0.0, OP.mult, OP.add)
+
+    def columns(rv, d0):
+        act(f(d0, 2, 1776, 3), f(rv, 0, 34, ind=("OUTL", 0, 37)), AF.Copy, -0.5 / UNIT)
+
+    def signs(d0):
+        act(f(d0, 1, 1776, 3), f(d0, 2, 1776, 3), AF.Sign)
+
+    def steps(dst, d0, src):
+        scan(f(dst, 0, 1734), f(d0, 0, 1734), f(src, 0, 1734), 0.0, OP.mult, OP.add)
+
+    for t in range(R):
+        ft = "F%d" % t
+        if t:
+            scores(t, "F%d" % (t - 1))
+            differences()
+            unpack(t)
+        scan(f("Z"), f("FOLD"), f("SG"), 0.0, OP.mult, OP.add)
+        choose(f("Z", 15, 544, 16), 0, "RSF")
+        for h in range(2):
+            ts(f("GT", ROW * h, ROW * h + ROW), f("RSF", BLK * h + 16, BLK * h + 289, 17), 0.0, OP.not_equal, -BIG, OP.mult)
+        tt(f("S2"), f("Z", 15, 544, 16), f("GT"), OP.add)
+        if t == 0:
+            more_constants()
+        clean(0, "RSF", "RVF", "SPF")
+        columns("RVF", "D0F")
+        choose(f("S2"), 2, "RSS")
+        if t == 0:
+            late_constants()
+        column(0, "RSF")
+        column(1, "RSS")
+        keys(0, "RSF")
+        for b in range(4):
+            ts(f("KL", 4 * b, 4 * b + 4), f("KC"), float(b), OP.add)
+        keys(1, "RSS")
+        act(f("KF"), f(ft, ind=("KL", 0, 16)))
+        scan(f("RK", 1, 153), f("KEY"), f("KEY"), -BIG, OP.max, OP.max)
+        scan(f("SK"), f("KEY"), f("RK", 0, 152), -BIG, OP.max, OP.min)
+        tt(f("DEC", 0, 8), f("RK", 19, 153, 19), f("ZK"), OP.max)
+        tt(f("DEC", 8, 16), f("SK", 18, 152, 19), f("ZK"), OP.max)
+        ts(f("DCM"), f("DEC"), 4095, OP.bitwise_and)
+        for b in range(4):
+            ts(f("LL", 16 * b, 16 * b + 16), f("DCM"), float(b), OP.add)
+        for b in range(4):
+            act(f("AB", 128 * b, 128 * b + 128), f(ft, ind=("LL", 16 * b, 16 * b + 8)))
+        rows("SPF", "TA", 0)
+        clean(1, "RSS", "RVS", "SPS")
+        act(f("SPA", 0, 578, 17), f("RVS", 0, 34), AF.Abs)
+        for j in range(2):
+            for h in range(2):
+                act(f("FG", 34 * j + ROW * h, 34 * j + ROW * h + ROW), f("YC", 0, ROW), AF.Abs, -1.0, f("IX", 2 * j + h, 2 * j + h + 1))
+        act(f("FS"), f("FG"), AF.Sign)
+        act(f("TA", 1, 1734, 3), f("TA", 0, 1734, 3), AF.Abs)
+        signs("D0F")
+        columns("RVS", "D0S")
+        signs("D0S")
+        for b in range(4):
+            tt(f("IO2", 128 * b, 128 * b + 128), f(ft, ind=("LL", 16 * b + 8, 16 * b + 16)), f("AB", 128 * b, 128 * b + 128), OP.add)
+        tt(f("FH"), f("FS", 0, 34), f("FS", 34, 68), OP.add)
+        for b in range(4):
+            tt(f("M2", 64 * b, 64 * b + 64), f("IO2", 128 * b, 128 * b + 64), f("IO2", 128 * b + 64, 128 * b + 128), OP.max)
+        ts(f("MH"), f("M2"), 0.5, OP.mult)
+        for b in range(4):
+            tt(f("YT", b, 256, 4), f("MH", 64 * b, 64 * b + 64), f("KF", 64 * b, 64 * b + 64), OP.subtract)
+        quant("SQ%d" % t, "SS%d" % t, 0, 128, f("YT"))
+        send(t)
+        steps("TB", "D0F", "TA")
+        rows("SPS", "TB", 0)
+        rows("SPA", "TB", 1)
+        act(f("FV", 0, 34), f("FH"), AF.Identity, 2.0, -3.0)
+        act(f("SPX", 0, 578, 17), f("FH"), AF.Identity, 2.0, -3.0)
+        act(f("D0X", 1, 1776, 3), f("FV", 0, 34, ind=("OUTL", 0, 37)))
+        act(f("YW"), f("YT", 0, 256), AF.Copy, 32.0)
+        steps("TC", "D0S", "TB")
+        rows("SPX", "D0X", 2)
+        ts(f("TD", 0, 1734, 3), f("TC", 2, 1734, 3), 3.0 * UNIT, OP.min, -3.0 * UNIT, OP.max)
+        steps("TA", "D0X", "TD")
+        for b in range(4):
+            mm(f("PS", 1024 + 512 * b, 1152 + 512 * b), f("WQ", 128 * b, 128 * b + 128), f("WS", 128 * b, 128 * b + 128), f("LQ%d" % t), f("LS%d" % t))
+        for b in range(4):
+            tt(f("V32", 64 * b, 64 * b + 64), f("PS", 1024 + 512 * b, 1088 + 512 * b), f("YW", b, 256, 4), OP.add)
+        ts(f("VV"), f("V32"), 0.03125, OP.mult)
+        cp(f(ft, ind=("KL", 0, 16)), f("VV"))
+
+    for a in range(2):
+        lo, hi = 256 * a, 256 * a + 256
+        quant("XQ3", "XS3", lo, hi, f("F2", 1024 * a, 1024 * a + 1024))
+        if a == 0:
+            quant("VQ", "VS", 0, 128, f("VT"))
+        mm(f("PS", 512 * a, 512 * a + 256), f("VQ"), f("VS"), f("XQ3", lo, hi), f("XS3", lo, hi))
+        dma("y", (T.oc[:, 4 * lo:4 * hi], []), f("XQ3", lo, hi, cast=dt.uint8))
+    ts(f("T1", 0, 1), pm, 3.0, OP.mult)
+    ts(f("QD", 0, 32), f("OLX"), pm, OP.is_equal, 1736.0, OP.mult)
+    ts(f("EM", 0, 32), f("OLI"), f("T1", 0, 1), OP.add)
+    tt(f("EE", 0, 32), f("EM", 0, 32), f("QD", 0, 32), OP.max)
+    cp(f("OL"), f("EE", 0, 32))
+    act(f("OAO"), f("TA", ind=("OL", 0, 32)), AF.Copy, -1.0 / UNIT)
+    cp(f("YO", 0, 256), f("PS", 0, 256))
+    cp(f("YO", 256, 512), f("PS", 512, 768))
+    dma("y", (T.y[:, 0:256], []), f("YO", 0, 256))
+    dma("s", (T.oa[:, :], []), f("OAO"))
+    dma("y", (T.y[:, 256:512], []), f("YO", 256, 512))
+    for k in range(4):
+        dma("s" if k % 2 else "y", (T.osc[4 * k:4 * k + 4, :], []), (T.XS3[32 * k:32 * k + 4, 0:512], [("XS3", 0, 512)]))
+    for sem in count:
+        if sem != "dma":
+            wait("p", sem, count[sem])

@@ -6,23 +6,24 @@ AF = ActivationFunctionType
 R = 3
 W = 2176
 ROW, BLK = 17, 323
+SEL = 2 * BLK
 UNIT = 131072.0
 BIG = 1.0e29
 
 CODES, PLANE, BF, F32, I32, U16 = "float8_e4m3fn_x4", "uint8", "bfloat16", "float32", "int32", "uint16"
 SCRATCH = {"PS": ("psum", [128, 3072], F32)}
 for _n, _w, _d in (
-    ("XT", 2048, BF), ("UT", 512, BF), ("VT", 512, BF), ("ET", 528, BF), ("ZT", 512, BF),
+    ("XT", 2048, BF), ("UT", 512, BF), ("VT", 512, BF), ("ET", 528, BF),
     ("UQ", 128, CODES), ("US", 128, PLANE), ("UQR", 128, CODES), ("USR", 128, PLANE), ("VQ", 128, CODES), ("VS", 128, PLANE),
-    ("WQ", 512, CODES), ("WS", 512, PLANE), ("EQ", 512, CODES), ("ES", 512, PLANE), ("ZQ", 128, CODES), ("ZS", 128, PLANE),
-    ("NDI", 32, I32), ("ARI", 512, I32), ("IA", 360, I32), ("FA", 400, F32),
-    ("ONE", 592, BF), ("IOT", 512, F32), ("KI", 512, F32), ("OWN", 512, F32),
+    ("WQ", 512, CODES), ("WS", 512, PLANE), ("EQ", 512, CODES), ("ES", 512, PLANE),
+    ("NDI", 32, I32), ("NDX", 32, I32), ("NDF", 32, F32), ("ARI", 512, I32), ("IA", 360, I32), ("FA", 400, F32),
+    ("ONE", 592, BF), ("KI", 512, F32), ("OWN", 512, F32),
     ("L32", 32, U16), ("UL", 8, U16), ("SL", 36, U16), ("AL", 38, U16), ("OUTL", 38, U16), ("OL", 32, U16),
-    ("G0", 512, F32), ("G1", 256, F32), ("G2", 128, F32), ("G3", 64, F32), ("N4", 32, F32), ("HL", 80, F32),
+    ("N4", 32, F32), ("HL", 80, F32),
     ("CM", 512, F32), ("PW", 528, F32), ("FOLD", 544, BF), ("YC", 323, BF), ("KEEP", 578, BF), ("RS0", 34, F32), ("RST", 34, F32),
-    ("SEG", 152, F32), ("PRI", 152, F32), ("CC", 152, F32), ("ZK", 8, F32), ("ARB", 528, BF),
-    ("SG", 544, F32), ("Z", 544, F32), ("RX", 34, F32), ("TT", 34, F32), ("IX", 4, F32), ("KAP", 646, BF), ("DM", 646, BF),
-    ("RSF", 646, BF), ("RSS", 646, BF), ("GT", 34, F32), ("S2", 34, F32), ("KEY", 152, F32), ("RK", 156, F32), ("SK", 152, F32),
+    ("SEG", 152, F32), ("PRI", 152, F32), ("CC", 152, F32), ("ZK", 16, F32), ("ARB", 528, BF),
+    ("SG", 544, F32), ("Z", 544, F32), ("RX", 34, F32), ("TT", 34, F32), ("IX", 4, F32), ("KAP", SEL, BF), ("DM", SEL, BF),
+    ("RS", 2 * SEL, BF), ("GT", 34, F32), ("S2", 34, F32), ("KEY", 152, F32), ("RK", 308, F32),
     ("DEC", 16, I32), ("DCM", 16, I32), ("LL", 64, U16), ("KC", 4, F32), ("KL", 16, U16),
     ("KF", 256, BF), ("AB", 512, BF), ("IO2", 512, BF), ("M2", 256, BF), ("MH", 256, BF), ("YT", 512, BF), ("YW", 256, BF),
     ("V32", 256, BF), ("VV", 256, BF), ("CLN", 68, BF), ("RVF", 48, BF), ("RVS", 48, BF), ("FV", 48, BF), ("FG", 68, BF),
@@ -33,7 +34,7 @@ for _n, _w, _d in (
   + tuple((n + "%d" % t, 512, d) for t in range(R + 1) for n, d in (("XQ", CODES), ("XS", PLANE))):
     SCRATCH[_n] = ("sbuf", [128, _w], _d)
 
-SEMAPHORES = ["cv", "cs", "ct", "cp", "left"] + ["arr%d" % t for t in range(R)] + ["dm%d" % i for i in range(40)]
+SEMAPHORES = ["cv", "cs", "ct", "cp", "left"] + ["arr%d" % t for t in range(R)] + ["dm%d" % i for i in range(48)]
 COUNTER = {"v": "cv", "s": "cs", "t": "ct", "p": "cp"}
 PART = {n: ("IA", a, w) for n, a, w in (("PI", 0, 1), ("PMI", 8, 1), ("ULI", 16, 8), ("EI", 24, 38), ("EE", 64, 38), ("EM", 104, 38), ("QD", 144, 38),
                                        ("OLI", 184, 32), ("OLX", 216, 32), ("NI", 248, 32), ("NHI", 280, 32), ("NLO", 312, 32))}
@@ -104,6 +105,7 @@ def make_tracker(g, T):
         eng[q].dma_start(out[0], in_[0]).then_inc(T.sem["dm%d" % n], 16)
         after("dma%d" % n, in_[1], out[1], "dm%d" % n, 16)
         count["dm%d" % n] = 16
+        return "dm%d" % n
 
     return view, wait, before, after, call, dma, count
 
@@ -162,13 +164,14 @@ def rank_program(g, core, T, topo):
     def affine(out, a, pattern, op, fillv, base, cm):
         call("p", lambda e: e.affine_select(out[0], a[0], pattern, op, fillv, base, cm), [out], [a])
 
-    def zeros(out, n):
-        iota(out, [[0, n]])
-
     dma("y", f("NDI"), (T.nd[:, :], []))
     dma("s", f("UT"), (T.u[:, :], []))
     dma("y", f("XT", 0, 1024), (T.x[:, 0:1024], []))
     dma("s", f("XT", 1024, 2048), (T.x[:, 1024:2048], []))
+    blocks = []
+    for i in range(16):
+        a, p, h = 32 * (i // 4), 16 * (i % 4 // 2), 16 * (i % 2)
+        blocks.append(dma("y" if i % 2 else "s", (T.NDX[a + p:a + p + 16, h:h + 16], []), (T.nd[a + h:a + h + 16, p:p + 16], [])))
     dma("y", f("ARI"), (T.ar[:, :], []))
     dma("s", f("WQ", cast=dt.uint8), (T.wc[:, :], []))
     dma("y", f("WS"), (T.ws[:, :], []))
@@ -179,32 +182,27 @@ def rank_program(g, core, T, topo):
     iota(f("PI"), [[0, 1]], 0, 1, small=False)
     iota(f("EI"), [[16, 38]], small=False)
     iota(f("KI"), [[1, 16], [0, 32]])
-    iota(f("IOT"), [[4, 512]])
     iota(f("ULI"), [[16, 8]], small=False)
+    affine(f("ET"), f("ONE", 0, 528), [[-1, 528]], OP.is_equal, 0.0, 3, 4)
     affine(f("FOLD"), f("ONE", 0, 544), [[0, 34], [1, 16]], OP.not_equal, 0.0, 0, 0)
     affine(f("RST"), f("RS0"), [[0, 2], [1, 17]], OP.not_equal, -BIG, 0, 0)
-    affine(f("ET"), f("ONE", 0, 528), [[-1, 528]], OP.is_equal, 0.0, 3, 4)
-    zeros(f("TA", 1734, 1784), 50)
+    iota(f("TA", 1734, 1784), [[0, 50]])
     iota(f("YC"), [[0, 19], [1, 17]])
     iota(f("SEG"), [[1, 8], [0, 19]], 1)
     iota(f("PRI"), [[0, 8], [-4096, 19]], 65536)
-    zeros(f("F0", 2048, W), 128)
-    zeros(f("YT", 256, 512), 256)
+    iota(f("F0", 2048, W), [[0, 128]])
+    iota(f("YT", 256, 512), [[0, 256]])
     affine(f("KEEP"), f("ONE", 0, 578), [[0, 34], [1, 17]], OP.not_equal, 0.0, 0, 0)
-    zeros(f("SPF"), 578)
-    zeros(f("D0F", 0, 1776, 3), 592)
-    zeros(f("SPS"), 578)
-    zeros(f("SPA"), 578)
-    zeros(f("D0S", 0, 1776, 3), 592)
-    zeros(f("SPX"), 578)
-    zeros(f("D0X", 0, 1776, 3), 592)
-    zeros(f("ZT"), 512)
-    for j in (1, 2):
-        zeros(f("TD", j, 1734, 3), 578)
     for t in range(1, R):
-        zeros(f("F%d" % t, 2048, W), 128)
+        iota(f("F%d" % t, 2048, W), [[0, 128]])
     iota(f("OLI"), [[867, 2], [51, 16]], 56, small=False)
     iota(f("OLX"), [[0, 2], [1, 16]], small=False)
+    for n in ("SPF", "SPS", "SPA", "SPX"):
+        act(f(n), f("ONE", 0, 578), AF.Copy, 0.0)
+    for n in ("D0F", "D0S", "D0X"):
+        act(f(n, 0, 1776, 3), f("ONE"), AF.Copy, 0.0)
+    for j in (1, 2):
+        act(f("TD", j, 1734, 3), f("ONE", 0, 578), AF.Copy, 0.0)
 
     ts(f("PMI"), f("PI"), 15, OP.bitwise_and)
     cp(f("PM"), f("PMI"))
@@ -214,25 +212,37 @@ def rank_program(g, core, T, topo):
     ts(f("QD"), f("EM"), 16, OP.logical_shift_right)
     ts(f("H17"), f("QD"), 17.0, OP.is_ge, 17.0, OP.mult)
     ts(f("T1"), f("QD"), -17.0, OP.mult)
+    ts(f("H256"), f("QD"), 17.0, OP.is_ge, 256.0, OP.mult)
     tt(f("XE"), f("QD"), f("H17"), OP.subtract)
     tt(f("YE"), f("T1"), f("EE"), OP.add)
+    ts(f("T2"), f("XE"), 16.0, OP.mult, -17.0, OP.add)
+    ts(f("T1"), f("XE"), 0.0, OP.is_equal, 1000.0, OP.mult)
+    ts(f("T3"), f("YE"), 0.0, OP.is_equal, 1000.0, OP.mult)
+    tt(f("T4"), f("XE"), f("T1"), OP.add)
+    tt(f("T5"), f("T1"), f("T3"), OP.add)
     ts(f("OWN"), f("KI"), pm, OP.is_equal)
     for h in range(2):
         cp(f("L32", h, 32, 2), f("NDI", 16 * h, 16 * h + 16))
+    cp(f("CM", ind=("L32", 0, 32)), f("OWN"))
+    tt(f("T1"), f("T2"), f("YE"), OP.add)
+    tt(f("T3"), f("H256"), f("T5"), OP.add)
+    tt(f("T2"), f("T4"), f("YE"), OP.is_equal)
     cp(f("UL"), f("ULI"))
-    tt(f("G0"), f("IOT", ind=("L32", 0, 32)), f("OWN"), OP.mult)
+    tt(f("T5"), f("T1"), f("T3"), OP.add)
+    ts(f("T4"), f("T2"), 520.0, OP.mult)
     quant("UQ", "US", 0, 128, f("UT"))
+    ts(f("T1"), f("T5"), 512.0, OP.min)
+    fill(f("SL"), 512)
     cp(f("UQR", cast=dt.uint32), f("UQ", cast=dt.uint32, ind=("UL", 0, 8)))
     cp(f("USR"), f("US", ind=("UL", 0, 8)))
-    tt(f("G1"), f("G0", 0, 256), f("G0", 256, 512), OP.add)
-    tt(f("G2"), f("G1", 0, 128), f("G1", 128, 256), OP.add)
-    tt(f("G3"), f("G2", 0, 64), f("G2", 64, 128), OP.add)
-    tt(f("N4"), f("G3", 0, 32), f("G3", 32, 64), OP.add)
-    cp(f("CM", ind=("L32", 0, 32)), f("OWN"))
-    fill(f("SL"), 512)
+    tt(f("T3"), f("T1"), f("T4"), OP.max)
+    fill(f("PW", 512, 528), -BIG / 32)
+    for s in blocks:
+        wait("v", s, 16)
+    ts(f("NDF"), f("NDX"), 4.0, OP.mult)
+    call("v", lambda e: e.transpose(T.N4[:, :], T.NDF[:, :]), [f("N4")], [f("NDF")])
     for h in range(2):
         ts(f("SL", 18 * h + 1, 18 * h + 17), f("N4", 16 * h, 16 * h + 16), 0.25, OP.mult)
-    fill(f("PW", 512, 528), -BIG / 32)
 
     def scores(t, src):
         for a in range(2):
@@ -251,47 +261,36 @@ def rank_program(g, core, T, topo):
 
     def differences():
         for h in range(2):
-            tt(f("DM", BLK * h, BLK * h + 289), f("TA", 867 * h + 2, 867 * h + 867, 3), f("TA", 867 * h + 5, 867 * h + 870, 3), OP.subtract)
+            scan(f("DM", BLK * h + 1, BLK * h + 289), f("TA", 867 * h + 2, 867 * h + 864, 3), f("TA", 867 * h + 8, 867 * h + 870, 3), 0.0, OP.subtract, OP.subtract)
 
     scores(0, "XT")
 
+    cp(f("AL"), f("T3"))
     ts(f("ARB", 0, 512), f("ARI"), -UNIT, OP.mult)
     fill(f("ARB", 512, 520), 0.0)
     fill(f("ARB", 520, 528), UNIT / 64)
-    ts(f("H256"), f("QD"), 17.0, OP.is_ge, 256.0, OP.mult)
-    ts(f("T1"), f("XE"), 0.0, OP.is_equal, 1000.0, OP.mult)
-    ts(f("T3"), f("YE"), 0.0, OP.is_equal, 1000.0, OP.mult)
-    ts(f("T2"), f("XE"), 16.0, OP.mult, -17.0, OP.add)
-    tt(f("T4"), f("XE"), f("T1"), OP.add)
-    tt(f("T5"), f("T1"), f("T3"), OP.add)
-    tt(f("T1"), f("T2"), f("YE"), OP.add)
-    tt(f("T3"), f("H256"), f("T5"), OP.add)
-    tt(f("T2"), f("T4"), f("YE"), OP.is_equal)
-    tt(f("T5"), f("T1"), f("T3"), OP.add)
-    ts(f("T4"), f("T2"), 520.0, OP.mult)
-    ts(f("T1"), f("T5"), 512.0, OP.min)
-    tt(f("T3"), f("T1"), f("T4"), OP.max)
-    cp(f("AL"), f("T3"))
     act(f("TA", 2, 1778, 3), f("ARB", ind=("AL", 0, 37)))
     for b in range(4):
         quant("EQ", "ES", 128 * b, 128 * b + 128, f("ET", 3 - b, 515 - b))
     unpack(0)
     cp(f("NI"), f("N4"))
+    fill(f("HL"), 0.0)
     ts(f("NHI"), f("NI"), 1920, OP.bitwise_and)
     ts(f("NLO"), f("NI"), 127, OP.bitwise_and)
-    fill(f("HL"), 0.0)
     for h in range(2):
         fill(f("HL", 36 * h, 36 * h + 1), 2048.0)
         ts(f("HL", 36 * h + 18, 36 * h + 19), pm, 4.0, OP.mult, 64.0 * h, OP.add)
         cp(f("HL", 36 * h + 1, 36 * h + 17), f("NHI", 16 * h, 16 * h + 16))
         cp(f("HL", 36 * h + 19, 36 * h + 35), f("NLO", 16 * h, 16 * h + 16))
+        fill(f("DM", BLK * h, BLK * h + 1), 0.0)
     for h in range(2):
         for j in range(2):
             tt(f("DM", BLK * h + 289 + 17 * j, BLK * h + 306 + 17 * j), f("HL", 36 * h + 18 * j, 36 * h + 18 * j + 17), f("HL", 36 * h + 18 * j + 1, 36 * h + 18 * j + 18), OP.subtract)
     differences()
 
     def late_constants():
-        ts(f("ZK"), f("SEG", 0, 152, 19), 1048576.0, OP.mult, 71680.0, OP.add)
+        for j in range(2):
+            ts(f("ZK", 8 * j, 8 * j + 8), f("SEG", 0, 152, 19), 1048576.0, OP.mult, 71680.0, OP.add)
         ts(f("CC"), f("SEG"), 1048576.0, OP.mult)
         tt(f("CC"), f("CC"), f("PRI"), OP.add)
         for s in range(8):
@@ -299,32 +298,32 @@ def rank_program(g, core, T, topo):
             tt(f("CC", a, a + 16), f("CC", a, a + 16), f("N4", 16 * (s % 2), 16 * (s % 2) + 16), OP.add)
         fill(f("RK", 0, 1), -BIG)
 
-    def more_constants():
-        tt(f("T2"), f("YE"), f("H17"), OP.add)
-        cp(f("OUTL"), f("T2"))
-        quant("ZQ", "ZS", 0, 128, f("ZT"))
-        for t in range(R):
-            dma("y", f("LQ%d" % t, 64, 128, cast=dt.uint8), f("ZQ", 64, 128, cast=dt.uint8))
-            dma("y", f("LS%d" % t, 64, 128), f("ZS", 64, 128))
+    def output_list():
+        ts(f("T1", 0, 1), pm, 3.0, OP.mult)
+        ts(f("QD", 0, 32), f("OLX"), pm, OP.is_equal, 1736.0, OP.mult)
+        ts(f("EM", 0, 32), f("OLI"), f("T1", 0, 1), OP.add)
+        tt(f("EE", 0, 32), f("EM", 0, 32), f("QD", 0, 32), OP.max)
+        cp(f("OL"), f("EE", 0, 32))
 
-    def choose(s, ix, out):
+    def choose(s, j):
         scan(f("RX"), f("RST"), s, 0.0, OP.min, OP.max)
         for h in range(2):
             ts(f("TT", ROW * h, ROW * h + ROW), f("RX", ROW * h, ROW * h + ROW), f("RX", ROW * h + 16, ROW * h + 17), OP.is_lt)
         for h in range(2):
-            total(f("IX", ix + h, ix + h + 1), f("TT", ROW * h, ROW * h + ROW))
+            total(f("IX", 2 * j + h, 2 * j + h + 1), f("TT", ROW * h, ROW * h + ROW))
         for h in range(2):
-            ts(f("KAP", BLK * h, BLK * h + BLK), f("YC"), f("IX", ix + h, ix + h + 1), OP.is_gt)
-        scan(f(out), f("KAP"), f("DM"), 0.0, OP.mult, OP.add)
+            ts(f("KAP", BLK * h, BLK * h + BLK), f("YC"), f("IX", 2 * j + h, 2 * j + h + 1), OP.is_gt)
+        scan(f("RS", SEL * j, SEL * j + SEL), f("KAP"), f("DM"), 0.0, OP.mult, OP.add)
 
-    def keys(j, rs):
-        r = f(rs, 16, 646, 17)
+    def keys(j):
+        r = f("RS", SEL * j + 16, SEL * j + SEL, 17)
         for io in range(2):
             a = 76 * io + 38 * j
             tt(f("KEY", a, a + 38), f("CC", a, a + 38), r, OP.add if io else OP.subtract)
 
-    def column(j, rs):
-        tt(f("KC", 2 * j, 2 * j + 2), f(rs, 305, 646, BLK), f(rs, 322, 646, BLK), OP.add)
+    def member_row(j, h):
+        at = SEL * j + BLK * h
+        return f("RS", at + 16, at + 289, 17)
 
     nxt = T.cores[(rank + 1) % len(T.cores)]
     rid, pid, _ = topo.addr(nxt)
@@ -340,9 +339,9 @@ def rank_program(g, core, T, topo):
         count["arr%d" % t] = 2 * engines
         count["left"] = count.get("left", 0) + 2 * engines
 
-    def clean(j, rs, rv, sp):
+    def clean(j, rv, sp):
         for h in range(2):
-            act(f("CLN", 34 * j + ROW * h, 34 * j + ROW * h + ROW), f(rs, BLK * h + 16, BLK * h + 289, 17), AF.Identity, 1.0 / UNIT, 192.0)
+            act(f("CLN", 34 * j + ROW * h, 34 * j + ROW * h + ROW), member_row(j, h), AF.Identity, 1.0 / UNIT, 192.0)
         act(f(rv, 0, 34), f("CLN", 34 * j, 34 * j + 34), AF.Identity, UNIT, -192.0 * UNIT)
         act(f(sp, 0, 578, 17), f("CLN", 34 * j, 34 * j + 34), AF.Identity, UNIT, -192.0 * UNIT)
 
@@ -351,8 +350,6 @@ def rank_program(g, core, T, topo):
 
     def columns(rv, d0):
         act(f(d0, 2, 1776, 3), f(rv, 0, 34, ind=("OUTL", 0, 37)), AF.Copy, -0.5 / UNIT)
-
-    def signs(d0):
         act(f(d0, 1, 1776, 3), f(d0, 2, 1776, 3), AF.Sign)
 
     def steps(dst, d0, src):
@@ -362,50 +359,47 @@ def rank_program(g, core, T, topo):
         ft = "F%d" % t
         if t:
             scores(t, "F%d" % (t - 1))
+            steps("TA", "D0X", "TD")
             differences()
             unpack(t)
         scan(f("Z"), f("FOLD"), f("SG"), 0.0, OP.mult, OP.add)
-        choose(f("Z", 15, 544, 16), 0, "RSF")
+        choose(f("Z", 15, 544, 16), 0)
         for h in range(2):
-            ts(f("GT", ROW * h, ROW * h + ROW), f("RSF", BLK * h + 16, BLK * h + 289, 17), 0.0, OP.not_equal, -BIG, OP.mult)
+            ts(f("GT", ROW * h, ROW * h + ROW), member_row(0, h), 0.0, OP.not_equal, -BIG, OP.mult)
         tt(f("S2"), f("Z", 15, 544, 16), f("GT"), OP.add)
         if t == 0:
-            more_constants()
-        clean(0, "RSF", "RVF", "SPF")
+            tt(f("T2"), f("YE"), f("H17"), OP.add)
+            cp(f("OUTL"), f("T2"))
+        clean(0, "RVF", "SPF")
         columns("RVF", "D0F")
-        choose(f("S2"), 2, "RSS")
+        choose(f("S2"), 1)
         if t == 0:
             late_constants()
-        column(0, "RSF")
-        column(1, "RSS")
-        keys(0, "RSF")
+        tt(f("KC"), f("RS", 305, 2 * SEL, BLK), f("RS", 322, 2 * SEL, BLK), OP.add)
+        keys(0)
         for b in range(4):
             ts(f("KL", 4 * b, 4 * b + 4), f("KC"), float(b), OP.add)
-        keys(1, "RSS")
+        keys(1)
         act(f("KF"), f(ft, ind=("KL", 0, 16)))
         scan(f("RK", 1, 153), f("KEY"), f("KEY"), -BIG, OP.max, OP.max)
-        scan(f("SK"), f("KEY"), f("RK", 0, 152), -BIG, OP.max, OP.min)
-        tt(f("DEC", 0, 8), f("RK", 19, 153, 19), f("ZK"), OP.max)
-        tt(f("DEC", 8, 16), f("SK", 18, 152, 19), f("ZK"), OP.max)
+        scan(f("RK", 153, 305), f("KEY"), f("RK", 0, 152), -BIG, OP.max, OP.min)
+        tt(f("DEC"), f("RK", 19, 305, 19), f("ZK"), OP.max)
         ts(f("DCM"), f("DEC"), 4095, OP.bitwise_and)
         for b in range(4):
             ts(f("LL", 16 * b, 16 * b + 16), f("DCM"), float(b), OP.add)
         for b in range(4):
             act(f("AB", 128 * b, 128 * b + 128), f(ft, ind=("LL", 16 * b, 16 * b + 8)))
         rows("SPF", "TA", 0)
-        clean(1, "RSS", "RVS", "SPS")
+        act(f("TA", 1, 1734, 3), f("TA", 0, 1734, 3), AF.Abs)
+        clean(1, "RVS", "SPS")
         act(f("SPA", 0, 578, 17), f("RVS", 0, 34), AF.Abs)
+        columns("RVS", "D0S")
         for j in range(2):
             for h in range(2):
                 act(f("FG", 34 * j + ROW * h, 34 * j + ROW * h + ROW), f("YC", 0, ROW), AF.Abs, -1.0, f("IX", 2 * j + h, 2 * j + h + 1))
         act(f("FS"), f("FG"), AF.Sign)
-        act(f("TA", 1, 1734, 3), f("TA", 0, 1734, 3), AF.Abs)
-        signs("D0F")
-        columns("RVS", "D0S")
-        signs("D0S")
         for b in range(4):
             tt(f("IO2", 128 * b, 128 * b + 128), f(ft, ind=("LL", 16 * b + 8, 16 * b + 16)), f("AB", 128 * b, 128 * b + 128), OP.add)
-        tt(f("FH"), f("FS", 0, 34), f("FS", 34, 68), OP.add)
         for b in range(4):
             tt(f("M2", 64 * b, 64 * b + 64), f("IO2", 128 * b, 128 * b + 64), f("IO2", 128 * b + 64, 128 * b + 128), OP.max)
         ts(f("MH"), f("M2"), 0.5, OP.mult)
@@ -413,7 +407,12 @@ def rank_program(g, core, T, topo):
             tt(f("YT", b, 256, 4), f("MH", 64 * b, 64 * b + 64), f("KF", 64 * b, 64 * b + 64), OP.subtract)
         quant("SQ%d" % t, "SS%d" % t, 0, 128, f("YT"))
         send(t)
+        if t == 0:
+            for i in range(R):
+                dma("y", f("LQ%d" % i, 64, 128, cast=dt.uint8), f("SQ0", 64, 128, cast=dt.uint8))
+                dma("y", f("LS%d" % i, 64, 128), f("SS0", 64, 128))
         steps("TB", "D0F", "TA")
+        tt(f("FH"), f("FS", 0, 34), f("FS", 34, 68), OP.add)
         rows("SPS", "TB", 0)
         rows("SPA", "TB", 1)
         act(f("FV", 0, 34), f("FH"), AF.Identity, 2.0, -3.0)
@@ -421,9 +420,14 @@ def rank_program(g, core, T, topo):
         act(f("D0X", 1, 1776, 3), f("FV", 0, 34, ind=("OUTL", 0, 37)))
         act(f("YW"), f("YT", 0, 256), AF.Copy, 32.0)
         steps("TC", "D0S", "TB")
-        rows("SPX", "D0X", 2)
         ts(f("TD", 0, 1734, 3), f("TC", 2, 1734, 3), 3.0 * UNIT, OP.min, -3.0 * UNIT, OP.max)
-        steps("TA", "D0X", "TD")
+        rows("SPX", "D0X", 2)
+        if t == R - 1:
+            output_list()
+            steps("TA", "D0X", "TD")
+            quant("VQ", "VS", 0, 128, f("VT"))
+            act(f("OAO"), f("TA", ind=("OL", 0, 32)), AF.Copy, -1.0 / UNIT)
+            dma("y", (T.oa[:, :], []), f("OAO"))
         for b in range(4):
             mm(f("PS", 1024 + 512 * b, 1152 + 512 * b), f("WQ", 128 * b, 128 * b + 128), f("WS", 128 * b, 128 * b + 128), f("LQ%d" % t), f("LS%d" % t))
         for b in range(4):
@@ -434,20 +438,11 @@ def rank_program(g, core, T, topo):
     for a in range(2):
         lo, hi = 256 * a, 256 * a + 256
         quant("XQ3", "XS3", lo, hi, f("F2", 1024 * a, 1024 * a + 1024))
-        if a == 0:
-            quant("VQ", "VS", 0, 128, f("VT"))
         mm(f("PS", 512 * a, 512 * a + 256), f("VQ"), f("VS"), f("XQ3", lo, hi), f("XS3", lo, hi))
         dma("y", (T.oc[:, 4 * lo:4 * hi], []), f("XQ3", lo, hi, cast=dt.uint8))
-    ts(f("T1", 0, 1), pm, 3.0, OP.mult)
-    ts(f("QD", 0, 32), f("OLX"), pm, OP.is_equal, 1736.0, OP.mult)
-    ts(f("EM", 0, 32), f("OLI"), f("T1", 0, 1), OP.add)
-    tt(f("EE", 0, 32), f("EM", 0, 32), f("QD", 0, 32), OP.max)
-    cp(f("OL"), f("EE", 0, 32))
-    act(f("OAO"), f("TA", ind=("OL", 0, 32)), AF.Copy, -1.0 / UNIT)
-    cp(f("YO", 0, 256), f("PS", 0, 256))
+    act(f("YO", 0, 256), f("PS", 0, 256))
+    dma("s", (T.y[:, 0:256], []), f("YO", 0, 256))
     cp(f("YO", 256, 512), f("PS", 512, 768))
-    dma("y", (T.y[:, 0:256], []), f("YO", 0, 256))
-    dma("s", (T.oa[:, :], []), f("OAO"))
     dma("y", (T.y[:, 256:512], []), f("YO", 256, 512))
     for k in range(4):
         dma("s" if k % 2 else "y", (T.osc[4 * k:4 * k + 4, :], []), (T.XS3[32 * k:32 * k + 4, 0:512], [("XS3", 0, 512)]))

@@ -7,6 +7,7 @@ R = 3
 W = 2176
 ROW, BLK = 17, 323
 SEL = 2 * BLK
+SQ3 = 867
 UNIT = 131072.0
 BIG = 1.0e29
 
@@ -55,12 +56,12 @@ def make_tracker(g, T):
         t = T[name]
         hi = int(t.shape[1]) if hi is None else hi
         ap = t[:, lo:hi:step] if step != 1 else t[:, lo:hi]
-        deps = [(name, lo, hi)]
+        deps = [(name, lo, hi, step)]
         if cast is not None:
             ap = ap.bitcast(cast)
         if ind is not None:
             ap = ap.indirect(T[ind[0]][:, ind[1]:ind[2]])
-            deps.append(ind)
+            deps.append((ind[0], ind[1], ind[2], 1))
         return ap, deps
 
     def wait(q, sem, val):
@@ -71,23 +72,23 @@ def make_tracker(g, T):
     def before(q, reads, writes):
         need = {}
         for acc, wr in ((reads, False), (writes, True)):
-            for name, lo, hi in acc:
-                for (a, b, w, sem, val, oq) in hist.get(name, []):
-                    if a < hi and lo < b and (w or wr):
+            for name, lo, hi, st in acc:
+                for (a, b, w, sem, val, oq, s2) in hist.get(name, []):
+                    if a < hi and lo < b and (w or wr) and (st != s2 or (lo - a) % st == 0):
                         need[sem] = max(need.get(sem, 0), val)
         for sem in need:
             wait(q, sem, need[sem])
 
     def after(q, reads, writes, sem, val):
-        for name, lo, hi in writes:
-            keep = [h for h in hist.get(name, []) if not (lo <= h[0] and h[1] <= hi)]
-            hist[name] = keep + [(lo, hi, True, sem, val, q)]
-        for name, lo, hi in reads:
-            keep = [h for h in hist.get(name, []) if h[2] or h[5] != q or not (lo <= h[0] and h[1] <= hi)]
-            hist[name] = keep + [(lo, hi, False, sem, val, q)]
+        def covered(h, lo, hi, st):
+            return lo <= h[0] and h[1] <= hi and (st == 1 or st == h[6] and (lo - h[0]) % st == 0)
+        for name, lo, hi, st in writes:
+            hist[name] = [h for h in hist.get(name, []) if not covered(h, lo, hi, st)] + [(lo, hi, True, sem, val, q, st)]
+        for name, lo, hi, st in reads:
+            hist[name] = [h for h in hist.get(name, []) if h[2] or h[5] != q or not covered(h, lo, hi, st)] + [(lo, hi, False, sem, val, q, st)]
 
     def bank(d):
-        return (d[0], d[1] // 512 * 512, (d[2] + 511) // 512 * 512) if d[0] == "PS" else d
+        return (d[0], d[1] // 512 * 512, (d[2] + 511) // 512 * 512, 1) if d[0] == "PS" else d
 
     def call(q, fn, outs, ins):
         reads = [d for v in ins for d in v[1] if d[0] != "PS"] + [d for v in outs for d in v[1][1:]]
@@ -191,8 +192,8 @@ def rank_program(g, core, T, topo):
     iota(f("SEG"), [[1, 8], [0, 19]], 1)
     iota(f("PRI"), [[0, 8], [-4096, 19]], 65536)
     iota(f("F0", 2048, W), [[0, 128]])
-    iota(f("YT", 256, 512), [[0, 256]])
     affine(f("KEEP"), f("ONE", 0, 578), [[0, 34], [1, 17]], OP.not_equal, 0.0, 0, 0)
+    iota(f("YT", 256, 512), [[0, 256]])
     for t in range(1, R):
         iota(f("F%d" % t, 2048, W), [[0, 128]])
     iota(f("OLI"), [[867, 2], [51, 16]], 56, small=False)
@@ -215,34 +216,34 @@ def rank_program(g, core, T, topo):
     ts(f("H256"), f("QD"), 17.0, OP.is_ge, 256.0, OP.mult)
     tt(f("XE"), f("QD"), f("H17"), OP.subtract)
     tt(f("YE"), f("T1"), f("EE"), OP.add)
-    ts(f("T2"), f("XE"), 16.0, OP.mult, -17.0, OP.add)
-    ts(f("T1"), f("XE"), 0.0, OP.is_equal, 1000.0, OP.mult)
-    ts(f("T3"), f("YE"), 0.0, OP.is_equal, 1000.0, OP.mult)
-    tt(f("T4"), f("XE"), f("T1"), OP.add)
-    tt(f("T5"), f("T1"), f("T3"), OP.add)
     ts(f("OWN"), f("KI"), pm, OP.is_equal)
     for h in range(2):
         cp(f("L32", h, 32, 2), f("NDI", 16 * h, 16 * h + 16))
+    ts(f("T1"), f("XE"), 0.0, OP.is_equal, 1000.0, OP.mult)
+    ts(f("T3"), f("YE"), 0.0, OP.is_equal, 1000.0, OP.mult)
     cp(f("CM", ind=("L32", 0, 32)), f("OWN"))
+    ts(f("T2"), f("XE"), 16.0, OP.mult, -17.0, OP.add)
+    tt(f("T4"), f("XE"), f("T1"), OP.add)
+    tt(f("T5"), f("T1"), f("T3"), OP.add)
+    cp(f("UL"), f("ULI"))
     tt(f("T1"), f("T2"), f("YE"), OP.add)
+    quant("UQ", "US", 0, 128, f("UT"))
     tt(f("T3"), f("H256"), f("T5"), OP.add)
     tt(f("T2"), f("T4"), f("YE"), OP.is_equal)
-    cp(f("UL"), f("ULI"))
-    tt(f("T5"), f("T1"), f("T3"), OP.add)
-    ts(f("T4"), f("T2"), 520.0, OP.mult)
-    quant("UQ", "US", 0, 128, f("UT"))
-    ts(f("T1"), f("T5"), 512.0, OP.min)
-    fill(f("SL"), 512)
     cp(f("UQR", cast=dt.uint32), f("UQ", cast=dt.uint32, ind=("UL", 0, 8)))
     cp(f("USR"), f("US", ind=("UL", 0, 8)))
-    tt(f("T3"), f("T1"), f("T4"), OP.max)
-    fill(f("PW", 512, 528), -BIG / 32)
     for s in blocks:
         wait("v", s, 16)
     ts(f("NDF"), f("NDX"), 4.0, OP.mult)
+    tt(f("T5"), f("T1"), f("T3"), OP.add)
+    ts(f("T4"), f("T2"), 520.0, OP.mult)
     call("v", lambda e: e.transpose(T.N4[:, :], T.NDF[:, :]), [f("N4")], [f("NDF")])
+    fill(f("SL", 0, 36, 18), 512)
+    fill(f("SL", 17, 18), 512)
+    fill(f("SL", 35, 36), 512)
     for h in range(2):
         ts(f("SL", 18 * h + 1, 18 * h + 17), f("N4", 16 * h, 16 * h + 16), 0.25, OP.mult)
+    fill(f("PW", 512, 528), -BIG / 32)
 
     def scores(t, src):
         for a in range(2):
@@ -259,44 +260,54 @@ def rank_program(g, core, T, topo):
         for b in range(4):
             act(f("F%d" % t, b, 2048, 4), f("PS", 1024 + 512 * b, 1536 + 512 * b))
 
-    def differences():
-        for h in range(2):
-            scan(f("DM", BLK * h + 1, BLK * h + 289), f("TA", 867 * h + 2, 867 * h + 864, 3), f("TA", 867 * h + 8, 867 * h + 870, 3), 0.0, OP.subtract, OP.subtract)
+    def differences(h):
+        scan(f("DM", BLK * h + 1, BLK * h + 289), f("TA", SQ3 * h + 2, SQ3 * h + 864, 3), f("TA", SQ3 * h + 8, SQ3 * h + 870, 3), 0.0, OP.subtract, OP.subtract)
 
     scores(0, "XT")
 
-    cp(f("AL"), f("T3"))
+    ts(f("T1"), f("T5"), 512.0, OP.min)
     ts(f("ARB", 0, 512), f("ARI"), -UNIT, OP.mult)
     fill(f("ARB", 512, 520), 0.0)
+    tt(f("T3"), f("T1"), f("T4"), OP.max)
     fill(f("ARB", 520, 528), UNIT / 64)
+    cp(f("NI"), f("N4"))
+    cp(f("AL"), f("T3"))
     act(f("TA", 2, 1778, 3), f("ARB", ind=("AL", 0, 37)))
+    fill(f("HL"), 0.0)
     for b in range(4):
         quant("EQ", "ES", 128 * b, 128 * b + 128, f("ET", 3 - b, 515 - b))
     unpack(0)
-    cp(f("NI"), f("N4"))
-    fill(f("HL"), 0.0)
     ts(f("NHI"), f("NI"), 1920, OP.bitwise_and)
     ts(f("NLO"), f("NI"), 127, OP.bitwise_and)
     for h in range(2):
         fill(f("HL", 36 * h, 36 * h + 1), 2048.0)
         ts(f("HL", 36 * h + 18, 36 * h + 19), pm, 4.0, OP.mult, 64.0 * h, OP.add)
+    for h in range(2):
         cp(f("HL", 36 * h + 1, 36 * h + 17), f("NHI", 16 * h, 16 * h + 16))
         cp(f("HL", 36 * h + 19, 36 * h + 35), f("NLO", 16 * h, 16 * h + 16))
+    for h in range(2):
         fill(f("DM", BLK * h, BLK * h + 1), 0.0)
     for h in range(2):
         for j in range(2):
             tt(f("DM", BLK * h + 289 + 17 * j, BLK * h + 306 + 17 * j), f("HL", 36 * h + 18 * j, 36 * h + 18 * j + 17), f("HL", 36 * h + 18 * j + 1, 36 * h + 18 * j + 18), OP.subtract)
-    differences()
 
-    def late_constants():
+    def outer_list():
+        tt(f("T2"), f("YE"), f("H17"), OP.add)
+        cp(f("OUTL"), f("T2"))
+
+    def bases():
+        ts(f("CC"), f("SEG"), 1048576.0, OP.mult)
         for j in range(2):
             ts(f("ZK", 8 * j, 8 * j + 8), f("SEG", 0, 152, 19), 1048576.0, OP.mult, 71680.0, OP.add)
-        ts(f("CC"), f("SEG"), 1048576.0, OP.mult)
+
+    def priorities():
         tt(f("CC"), f("CC"), f("PRI"), OP.add)
-        for s in range(8):
+        fill(f("RK", 0, 1), -BIG)
+
+    def member_columns(lo):
+        for s in range(lo, lo + 4):
             a = 19 * s + 1
             tt(f("CC", a, a + 16), f("CC", a, a + 16), f("N4", 16 * (s % 2), 16 * (s % 2) + 16), OP.add)
-        fill(f("RK", 0, 1), -BIG)
 
     def output_list():
         ts(f("T1", 0, 1), pm, 3.0, OP.mult)
@@ -305,21 +316,28 @@ def rank_program(g, core, T, topo):
         tt(f("EE", 0, 32), f("EM", 0, 32), f("QD", 0, 32), OP.max)
         cp(f("OL"), f("EE", 0, 32))
 
-    def choose(s, j):
-        scan(f("RX"), f("RST"), s, 0.0, OP.min, OP.max)
+    def choose(s, j, slots):
+        def slot():
+            if slots:
+                slots.pop(0)()
+        for h in range(2):
+            scan(f("RX", ROW * h, ROW * h + ROW), f("RST", 0, ROW), s(h), 0.0, OP.min, OP.max)
+        slot()
         for h in range(2):
             ts(f("TT", ROW * h, ROW * h + ROW), f("RX", ROW * h, ROW * h + ROW), f("RX", ROW * h + 16, ROW * h + 17), OP.is_lt)
+        slot()
         for h in range(2):
             total(f("IX", 2 * j + h, 2 * j + h + 1), f("TT", ROW * h, ROW * h + ROW))
+        slot()
         for h in range(2):
             ts(f("KAP", BLK * h, BLK * h + BLK), f("YC"), f("IX", 2 * j + h, 2 * j + h + 1), OP.is_gt)
-        scan(f("RS", SEL * j, SEL * j + SEL), f("KAP"), f("DM"), 0.0, OP.mult, OP.add)
+        for h in range(2):
+            at = SEL * j + BLK * h
+            scan(f("RS", at, at + BLK), f("KAP", BLK * h, BLK * h + BLK), f("DM", BLK * h, BLK * h + BLK), 0.0, OP.mult, OP.add)
 
-    def keys(j):
-        r = f("RS", SEL * j + 16, SEL * j + SEL, 17)
-        for io in range(2):
-            a = 76 * io + 38 * j
-            tt(f("KEY", a, a + 38), f("CC", a, a + 38), r, OP.add if io else OP.subtract)
+    def key(j, io):
+        a = 76 * io + 38 * j
+        tt(f("KEY", a, a + 38), f("CC", a, a + 38), f("RS", SEL * j + 16, SEL * j + SEL, 17), OP.add if io else OP.subtract)
 
     def member_row(j, h):
         at = SEL * j + BLK * h
@@ -335,97 +353,136 @@ def rank_program(g, core, T, topo):
         before("p", q[1] + s[1], [])
         g.remote_dma(T["LQ%d" % t][:, 0:64].bitcast(dt.uint8), q[0], T.sem["arr%d" % t], T.sem["left"], pid, rid, mask)
         g.remote_dma(T["LS%d" % t][:, 0:64], s[0], T.sem["arr%d" % t], T.sem["left"], pid, rid, mask)
-        after("in%d" % t, [], [("LQ%d" % t, 0, 64), ("LS%d" % t, 0, 64)], "arr%d" % t, 2 * engines)
+        after("in%d" % t, [], [("LQ%d" % t, 0, 64, 1), ("LS%d" % t, 0, 64, 1)], "arr%d" % t, 2 * engines)
         count["arr%d" % t] = 2 * engines
         count["left"] = count.get("left", 0) + 2 * engines
 
-    def clean(j, rv, sp):
+    def clean(j):
         for h in range(2):
             act(f("CLN", 34 * j + ROW * h, 34 * j + ROW * h + ROW), member_row(j, h), AF.Identity, 1.0 / UNIT, 192.0)
-        act(f(rv, 0, 34), f("CLN", 34 * j, 34 * j + 34), AF.Identity, UNIT, -192.0 * UNIT)
-        act(f(sp, 0, 578, 17), f("CLN", 34 * j, 34 * j + 34), AF.Identity, UNIT, -192.0 * UNIT)
 
-    def rows(sp, out, lo):
-        scan(f(out, lo, 1734, 3), f("KEEP"), f(sp), 0.0, OP.mult, OP.add)
+    def scaled(j, out):
+        act(out, f("CLN", 34 * j, 34 * j + 34), AF.Identity, UNIT, -192.0 * UNIT)
+
+    def place_marks(j):
+        for h in range(2):
+            act(f("FG", 34 * j + ROW * h, 34 * j + ROW * h + ROW), f("YC", 0, ROW), AF.Abs, -1.0, f("IX", 2 * j + h, 2 * j + h + 1))
+
+    def rows(sp, out, lo, h):
+        scan(f(out, lo + SQ3 * h, SQ3 * h + SQ3, 3), f("KEEP", 0, 289), f(sp, 289 * h, 289 * h + 289), 0.0, OP.mult, OP.add)
 
     def columns(rv, d0):
         act(f(d0, 2, 1776, 3), f(rv, 0, 34, ind=("OUTL", 0, 37)), AF.Copy, -0.5 / UNIT)
+
+    def column_signs(d0):
         act(f(d0, 1, 1776, 3), f(d0, 2, 1776, 3), AF.Sign)
 
-    def steps(dst, d0, src):
-        scan(f(dst, 0, 1734), f(d0, 0, 1734), f(src, 0, 1734), 0.0, OP.mult, OP.add)
+    def steps(dst, d0, src, h):
+        lo, hi = SQ3 * h, SQ3 * h + SQ3
+        scan(f(dst, lo, hi), f(d0, lo, hi), f(src, lo, hi), 0.0, OP.mult, OP.add)
 
     for t in range(R):
         ft = "F%d" % t
         if t:
             scores(t, "F%d" % (t - 1))
-            steps("TA", "D0X", "TD")
-            differences()
+            for h in range(2):
+                steps("TA", "D0X", "TD", h)
             unpack(t)
-        scan(f("Z"), f("FOLD"), f("SG"), 0.0, OP.mult, OP.add)
-        choose(f("Z", 15, 544, 16), 0)
+        for h in range(2):
+            scan(f("Z", 272 * h, 272 * h + 272), f("FOLD", 0, 272), f("SG", 272 * h, 272 * h + 272), 0.0, OP.mult, OP.add)
+        choose(lambda h: f("Z", 272 * h + 15, 272 * h + 272, 16), 0, [lambda: differences(0), lambda: differences(1)] + ([outer_list] if t == 0 else []))
         for h in range(2):
             ts(f("GT", ROW * h, ROW * h + ROW), member_row(0, h), 0.0, OP.not_equal, -BIG, OP.mult)
-        tt(f("S2"), f("Z", 15, 544, 16), f("GT"), OP.add)
-        if t == 0:
-            tt(f("T2"), f("YE"), f("H17"), OP.add)
-            cp(f("OUTL"), f("T2"))
-        clean(0, "RVF", "SPF")
+        clean(0)
+        scaled(0, f("RVF", 0, 34))
+        scaled(0, f("SPF", 0, 578, 17))
         columns("RVF", "D0F")
-        choose(f("S2"), 1)
+        column_signs("D0F")
         if t == 0:
-            late_constants()
+            bases()
+        for h in range(2):
+            tt(f("S2", ROW * h, ROW * h + ROW), f("Z", 272 * h + 15, 272 * h + 272, 16), f("GT", ROW * h, ROW * h + ROW), OP.add)
+        if t == 0:
+            choose(lambda h: f("S2", ROW * h, ROW * h + ROW), 1, [priorities, lambda: member_columns(0), lambda: member_columns(4)])
+            key(0, 0)
+            key(0, 1)
+        else:
+            choose(lambda h: f("S2", ROW * h, ROW * h + ROW), 1, [lambda: key(0, 0), lambda: key(0, 1)])
+        rows("SPF", "TA", 0, 0)
         tt(f("KC"), f("RS", 305, 2 * SEL, BLK), f("RS", 322, 2 * SEL, BLK), OP.add)
-        keys(0)
+        key(1, 0)
+        key(1, 1)
         for b in range(4):
             ts(f("KL", 4 * b, 4 * b + 4), f("KC"), float(b), OP.add)
-        keys(1)
         act(f("KF"), f(ft, ind=("KL", 0, 16)))
-        scan(f("RK", 1, 153), f("KEY"), f("KEY"), -BIG, OP.max, OP.max)
-        scan(f("RK", 153, 305), f("KEY"), f("RK", 0, 152), -BIG, OP.max, OP.min)
-        tt(f("DEC"), f("RK", 19, 305, 19), f("ZK"), OP.max)
-        ts(f("DCM"), f("DEC"), 4095, OP.bitwise_and)
+        for io in range(2):
+            scan(f("RK", 76 * io + 1, 76 * io + 77), f("KEY", 76 * io, 76 * io + 76), f("KEY", 76 * io, 76 * io + 76), -BIG, OP.max, OP.max)
+        scan(f("RK", 153, 229), f("KEY", 0, 76), f("RK", 0, 76), -BIG, OP.max, OP.min)
+        tt(f("DEC", 0, 8), f("RK", 19, 153, 19), f("ZK", 0, 8), OP.max)
+        scan(f("RK", 229, 305), f("KEY", 76, 152), f("RK", 76, 152), -BIG, OP.max, OP.min)
+        ts(f("DCM", 0, 8), f("DEC", 0, 8), 4095, OP.bitwise_and)
+        tt(f("DEC", 8, 16), f("RK", 171, 305, 19), f("ZK", 8, 16), OP.max)
         for b in range(4):
-            ts(f("LL", 16 * b, 16 * b + 16), f("DCM"), float(b), OP.add)
+            ts(f("LL", 8 * b, 8 * b + 8), f("DCM", 0, 8), float(b), OP.add)
+            act(f("AB", 128 * b, 128 * b + 128), f(ft, ind=("LL", 8 * b, 8 * b + 8)))
+            if b == 1:
+                ts(f("DCM", 8, 16), f("DEC", 8, 16), 4095, OP.bitwise_and)
         for b in range(4):
-            act(f("AB", 128 * b, 128 * b + 128), f(ft, ind=("LL", 16 * b, 16 * b + 8)))
-        rows("SPF", "TA", 0)
-        act(f("TA", 1, 1734, 3), f("TA", 0, 1734, 3), AF.Abs)
-        clean(1, "RVS", "SPS")
+            ts(f("LL", 32 + 8 * b, 40 + 8 * b), f("DCM", 8, 16), float(b), OP.add)
+        rows("SPF", "TA", 0, 1)
+        clean(1)
+        place_marks(0)
+        scaled(1, f("RVS", 0, 34))
+        scaled(1, f("SPS", 0, 578, 17))
+        place_marks(1)
         act(f("SPA", 0, 578, 17), f("RVS", 0, 34), AF.Abs)
-        columns("RVS", "D0S")
-        for j in range(2):
-            for h in range(2):
-                act(f("FG", 34 * j + ROW * h, 34 * j + ROW * h + ROW), f("YC", 0, ROW), AF.Abs, -1.0, f("IX", 2 * j + h, 2 * j + h + 1))
+        act(f("TA", 1, 1734, 3), f("TA", 0, 1734, 3), AF.Abs)
         act(f("FS"), f("FG"), AF.Sign)
+        columns("RVS", "D0S")
+        column_signs("D0S")
         for b in range(4):
-            tt(f("IO2", 128 * b, 128 * b + 128), f(ft, ind=("LL", 16 * b + 8, 16 * b + 16)), f("AB", 128 * b, 128 * b + 128), OP.add)
-        for b in range(4):
+            tt(f("IO2", 128 * b, 128 * b + 128), f(ft, ind=("LL", 32 + 8 * b, 40 + 8 * b)), f("AB", 128 * b, 128 * b + 128), OP.add)
+
+        def larger(b):
             tt(f("M2", 64 * b, 64 * b + 64), f("IO2", 128 * b, 128 * b + 64), f("IO2", 128 * b + 64, 128 * b + 128), OP.max)
-        ts(f("MH"), f("M2"), 0.5, OP.mult)
-        for b in range(4):
+
+        def half(a):
+            ts(f("MH", 128 * a, 128 * a + 128), f("M2", 128 * a, 128 * a + 128), 0.5, OP.mult)
+
+        def less(b):
             tt(f("YT", b, 256, 4), f("MH", 64 * b, 64 * b + 64), f("KF", 64 * b, 64 * b + 64), OP.subtract)
+
+        for fn, b in ((larger, 0), (larger, 1), (larger, 2), (half, 0), (larger, 3), (less, 0), (half, 1), (less, 1), (less, 2), (less, 3)):
+            fn(b)
         quant("SQ%d" % t, "SS%d" % t, 0, 128, f("YT"))
         send(t)
         if t == 0:
             for i in range(R):
                 dma("y", f("LQ%d" % i, 64, 128, cast=dt.uint8), f("SQ0", 64, 128, cast=dt.uint8))
                 dma("y", f("LS%d" % i, 64, 128), f("SS0", 64, 128))
-        steps("TB", "D0F", "TA")
+        for h in range(2):
+            steps("TB", "D0F", "TA", h)
         tt(f("FH"), f("FS", 0, 34), f("FS", 34, 68), OP.add)
-        rows("SPS", "TB", 0)
-        rows("SPA", "TB", 1)
         act(f("FV", 0, 34), f("FH"), AF.Identity, 2.0, -3.0)
         act(f("SPX", 0, 578, 17), f("FH"), AF.Identity, 2.0, -3.0)
         act(f("D0X", 1, 1776, 3), f("FV", 0, 34, ind=("OUTL", 0, 37)))
         act(f("YW"), f("YT", 0, 256), AF.Copy, 32.0)
-        steps("TC", "D0S", "TB")
-        ts(f("TD", 0, 1734, 3), f("TC", 2, 1734, 3), 3.0 * UNIT, OP.min, -3.0 * UNIT, OP.max)
-        rows("SPX", "D0X", 2)
-        if t == R - 1:
+        for h in range(2):
+            rows("SPS", "TB", 0, h)
+        for h in range(2):
+            rows("SPA", "TB", 1, h)
+        for h in range(2):
+            steps("TC", "D0S", "TB", h)
+        rows("SPX", "D0X", 2, 0)
+        for h in range(2):
+            ts(f("TD", SQ3 * h, SQ3 * h + SQ3, 3), f("TC", SQ3 * h + 2, SQ3 * h + SQ3, 3), 3.0 * UNIT, OP.min, -3.0 * UNIT, OP.max)
+        if t == 1:
             output_list()
-            steps("TA", "D0X", "TD")
+        if t == R - 1:
+            rows("SPX", "D0X", 2, 1)
             quant("VQ", "VS", 0, 128, f("VT"))
+            for h in range(2):
+                steps("TA", "D0X", "TD", h)
             act(f("OAO"), f("TA", ind=("OL", 0, 32)), AF.Copy, -1.0 / UNIT)
             dma("y", (T.oa[:, :], []), f("OAO"))
         for b in range(4):
@@ -433,6 +490,8 @@ def rank_program(g, core, T, topo):
         for b in range(4):
             tt(f("V32", 64 * b, 64 * b + 64), f("PS", 1024 + 512 * b, 1088 + 512 * b), f("YW", b, 256, 4), OP.add)
         ts(f("VV"), f("V32"), 0.03125, OP.mult)
+        if t < R - 1:
+            rows("SPX", "D0X", 2, 1)
         cp(f(ft, ind=("KL", 0, 16)), f("VV"))
 
     for a in range(2):
@@ -445,7 +504,7 @@ def rank_program(g, core, T, topo):
     cp(f("YO", 256, 512), f("PS", 512, 768))
     dma("y", (T.y[:, 256:512], []), f("YO", 256, 512))
     for k in range(4):
-        dma("s" if k % 2 else "y", (T.osc[4 * k:4 * k + 4, :], []), (T.XS3[32 * k:32 * k + 4, 0:512], [("XS3", 0, 512)]))
+        dma("s" if k % 2 else "y", (T.osc[4 * k:4 * k + 4, :], []), (T.XS3[32 * k:32 * k + 4, 0:512], [("XS3", 0, 512, 1)]))
     for sem in count:
         if sem != "dma":
             wait("p", sem, count[sem])

from concourse.bass import DstId, RemoteDMATransfer
from concourse.mybir import dt, AluOpType, AxisListType, ActivationFunctionType

OP = AluOpType
AF = ActivationFunctionType
R = 3
W = 2176
ROW, BLK = 17, 323
SEL = 2 * BLK
SQ3 = 867
UNIT = 131072.0
BIG = 1.0e29

CODES, PLANE, BF, F32, I32, U16 = "float8_e4m3fn_x4", "uint8", "bfloat16", "float32", "int32", "uint16"
SCRATCH = {"PS": ("psum", [128, 3072], F32)}
for _n, _w, _d in (
    ("XT", 2048, BF), ("UT", 512, BF), ("VT", 512, BF), ("ET", 528, BF),
    ("UQ", 128, CODES), ("US", 128, PLANE), ("UQR", 128, CODES), ("USR", 128, PLANE), ("VQ", 128, CODES), ("VS", 128, PLANE),
    ("WQ", 512, CODES), ("WS", 512, PLANE), ("EQ", 512, CODES), ("ES", 512, PLANE),
    ("NDI", 32, I32), ("NDX", 32, I32), ("NDF", 32, F32), ("ARI", 512, I32), ("IA", 360, I32), ("FA", 400, F32),
    ("ONE", 592, BF), ("KI", 512, F32), ("OWN", 512, F32),
    ("L32", 32, U16), ("UL", 8, U16), ("SL", 36, U16), ("AL", 38, U16), ("OUTL", 38, U16), ("OL", 32, U16),
    ("N4", 32, F32), ("HL", 80, F32),
    ("CM", 512, F32), ("PW", 528, F32), ("FOLD", 544, BF), ("YC", 323, BF), ("KEEP", 578, BF), ("RS0", 34, F32), ("RST", 34, F32),
    ("SEG", 152, F32), ("PRI", 152, F32), ("CC", 152, F32), ("ZK", 16, F32), ("ARB", 528, BF),
    ("SG", 544, F32), ("Z", 544, F32), ("RX", 34, F32), ("TT", 34, F32), ("IX", 4, F32), ("KAP", SEL, BF), ("DM", SEL, BF),
    ("RS", 2 * SEL, BF), ("GT", 34, F32), ("S2", 34, F32), ("KEY", 152, F32), ("RK", 308, F32),
    ("DEC", 16, I32), ("DCM", 16, I32), ("LL", 64, U16), ("KC", 4, F32), ("KL", 16, U16),
    ("KF", 256, BF), ("AB", 512, BF), ("IO2", 512, BF), ("M2", 256, BF), ("MH", 256, BF), ("YT", 512, BF), ("YW", 256, BF),
    ("V32", 256, BF), ("VV", 256, BF), ("CLN", 68, BF), ("RVF", 48, BF), ("RVS", 48, BF), ("FV", 48, BF), ("FG", 68, BF),
    ("FS", 68, BF), ("FH", 34, BF), ("SPF", 578, BF), ("SPS", 578, BF), ("SPA", 578, BF), ("SPX", 578, BF),
    ("D0F", 1776, BF), ("D0S", 1776, BF), ("D0X", 1776, BF), ("TA", 1784, BF), ("TB", 1744, BF), ("TC", 1744, BF), ("TD", 1744, BF),
    ("OAO", 512, F32), ("YO", 512, F32),
) + tuple(("F%d" % t, W, BF) for t in range(R)) + tuple((n + "%d" % t, 128, d) for t in range(R) for n, d in (("SQ", CODES), ("SS", PLANE), ("LQ", CODES), ("LS", PLANE))) \
  + tuple((n + "%d" % t, 512, d) for t in range(R + 1) for n, d in (("XQ", CODES), ("XS", PLANE))):
    SCRATCH[_n] = ("sbuf", [128, _w], _d)

SEMAPHORES = ["cv", "cs", "ct", "cp", "left"] + ["arr%d" % t for t in range(R)] + ["dm%d" % i for i in range(48)]
COUNTER = {"v": "cv", "s": "cs", "t": "ct", "p": "cp"}
PART = {n: ("IA", a, w) for n, a, w in (("PI", 0, 1), ("PMI", 8, 1), ("ULI", 16, 8), ("EI", 24, 38), ("EE", 64, 38), ("EM", 104, 38), ("QD", 144, 38),
                                       ("OLI", 184, 32), ("OLX", 216, 32), ("NI", 248, 32), ("NHI", 280, 32), ("NLO", 312, 32))}
PART.update({n: ("FA", a, w) for n, a, w in (("PM", 0, 1), ("H17", 8, 38), ("H256", 48, 38), ("YE", 88, 38), ("XE", 128, 38), ("T1", 168, 38),
                                            ("T2", 208, 38), ("T3", 248, 38), ("T4", 288, 38), ("T5", 328, 38))})


def make_tracker(g, T):
    eng = {"v": g.vector, "s": g.scalar, "t": g.tensor, "p": g, "y": g.sync}
    count = {}
    known = {q: {} for q in eng}
    hist = {}

    def view(name, lo=0, hi=None, step=1, ind=None, cast=None):
        if name in PART:
            name, at, width = PART[name]
            lo, hi = lo + at, (width if hi is None else hi) + at
        t = T[name]
        hi = int(t.shape[1]) if hi is None else hi
        ap = t[:, lo:hi:step] if step != 1 else t[:, lo:hi]
        deps = [(name, lo, hi, step)]
        if cast is not None:
            ap = ap.bitcast(cast)
        if ind is not None:
            ap = ap.indirect(T[ind[0]][:, ind[1]:ind[2]])
            deps.append((ind[0], ind[1], ind[2], 1))
        return ap, deps

    def wait(q, sem, val):
        if known[q].get(sem, 0) < val:
            known[q][sem] = val
            eng[q].wait_ge(T.sem[sem], val)

    def before(q, reads, writes):
        need = {}
        for acc, wr in ((reads, False), (writes, True)):
            for name, lo, hi, st in acc:
                for (a, b, w, sem, val, oq, s2) in hist.get(name, []):
                    if a < hi and lo < b and (w or wr) and (st != s2 or (lo - a) % st == 0):
                        need[sem] = max(need.get(sem, 0), val)
        for sem in need:
            wait(q, sem, need[sem])

    def after(q, reads, writes, sem, val):
        def covered(h, lo, hi, st):
            return lo <= h[0] and h[1] <= hi and (st == 1 or st == h[6] and (lo - h[0]) % st == 0)
        for name, lo, hi, st in writes:
            hist[name] = [h for h in hist.get(name, []) if not covered(h, lo, hi, st)] + [(lo, hi, True, sem, val, q, st)]
        for name, lo, hi, st in reads:
            hist[name] = [h for h in hist.get(name, []) if h[2] or h[5] != q or not covered(h, lo, hi, st)] + [(lo, hi, False, sem, val, q, st)]

    def bank(d):
        return (d[0], d[1] // 512 * 512, (d[2] + 511) // 512 * 512, 1) if d[0] == "PS" else d

    def call(q, fn, outs, ins):
        reads = [d for v in ins for d in v[1] if d[0] != "PS"] + [d for v in outs for d in v[1][1:]]
        writes = [bank(v[1][0]) for v in outs] + [bank(d) for v in ins for d in v[1] if d[0] == "PS"]
        before(q, reads, writes)
        sem = COUNTER[q]
        count[sem] = count.get(sem, 0) + 1
        fn(eng[q]).then_inc(T.sem[sem], 1)
        after(q, reads, writes, sem, count[sem])

    def dma(q, out, in_):
        before(q, in_[1], out[1])
        n = count.get("dma", 0)
        count["dma"] = n + 1
        eng[q].dma_start(out[0], in_[0]).then_inc(T.sem["dm%d" % n], 16)
        after("dma%d" % n, in_[1], out[1], "dm%d" % n, 16)
        count["dm%d" % n] = 16
        return "dm%d" % n

    return view, wait, before, after, call, dma, count


def rank_program(g, core, T, topo):
    rank = T.rank_of(core)
    if rank is None:
        return
    f, wait, before, after, call, dma, count = make_tracker(g, T)

    def tt(out, a, b, op):
        call("v", lambda e: e.tensor_tensor(out[0], a[0], b[0], op), [out], [a, b])

    def ts(out, a, s1, op0, s2=None, op1=None):
        ins = [a] + [s for s in (s1, s2) if isinstance(s, tuple)]
        x1 = s1[0] if isinstance(s1, tuple) else s1
        x2 = s2[0] if isinstance(s2, tuple) else s2
        if op1 is None:
            call("v", lambda e: e.tensor_scalar(out[0], a[0], x1, None, op0), [out], ins)
        else:
            call("v", lambda e: e.tensor_scalar(out[0], a[0], x1, x2, op0, op1), [out], ins)

    def cp(out, a):
        call("v", lambda e: e.tensor_copy(out[0], a[0]), [out], [a])

    def fill(out, c):
        call("v", lambda e: e.memset(out[0], c), [out], [])

    def scan(out, d0, d1, init, op0, op1):
        call("v", lambda e: e.tensor_tensor_scan(out[0], d0[0], d1[0], init, op0, op1), [out], [d0, d1])

    def total(out, a):
        call("v", lambda e: e.tensor_reduce(out[0], a[0], AxisListType.X, OP.add), [out], [a])

    def quant(qn, sn, lo, hi, a):
        q, s = f(qn, lo, hi), f(sn, lo, hi)
        call("v", lambda e: e.quantize_mx(q[0], s[0], a[0]), [q, s], [a])

    def act(out, a, func=AF.Copy, scale=1.0, bias=None):
        if bias is None:
            call("s", lambda e: e.activation(out[0], a[0], func, scale=scale), [out], [a])
        elif isinstance(bias, tuple):
            call("s", lambda e: e.activation(out[0], a[0], func, bias=bias[0], scale=scale), [out], [a, bias])
        else:
            call("s", lambda e: e.activation(out[0], a[0], func, bias=bias, scale=scale), [out], [a])

    def mm(out, l, ls, r, rs):
        call("t", lambda e: e.matmul_mx(out[0], l[0], ls[0], r[0], rs[0], True, True), [out], [l, ls, r, rs])

    def iota(out, pattern, base=0, cm=0, small=True):
        if small:
            call("p", lambda e: e.iota(out[0], pattern, base, cm, allow_small_or_imprecise_dtypes=True), [out], [])
        else:
            call("p", lambda e: e.iota(out[0], pattern, base, cm), [out], [])

    def affine(out, a, pattern, op, fillv, base, cm):
        call("p", lambda e: e.affine_select(out[0], a[0], pattern, op, fillv, base, cm), [out], [a])

    dma("y", f("NDI"), (T.nd[:, :], []))
    dma("s", f("UT"), (T.u[:, :], []))
    dma("y", f("XT", 0, 1024), (T.x[:, 0:1024], []))
    dma("s", f("XT", 1024, 2048), (T.x[:, 1024:2048], []))
    blocks = []
    for i in range(16):
        a, p, h = 32 * (i // 4), 16 * (i % 4 // 2), 16 * (i % 2)
        blocks.append(dma("y" if i % 2 else "s", (T.NDX[a + p:a + p + 16, h:h + 16], []), (T.nd[a + h:a + h + 16, p:p + 16], [])))
    dma("y", f("ARI"), (T.ar[:, :], []))
    dma("s", f("WQ", cast=dt.uint8), (T.wc[:, :], []))
    dma("y", f("WS"), (T.ws[:, :], []))
    dma("s", f("VT"), (T.v[:, :], []))

    fill(f("ONE"), 1.0)
    fill(f("RS0"), BIG)
    iota(f("PI"), [[0, 1]], 0, 1, small=False)
    iota(f("EI"), [[16, 38]], small=False)
    iota(f("KI"), [[1, 16], [0, 32]])
    iota(f("ULI"), [[16, 8]], small=False)
    affine(f("ET"), f("ONE", 0, 528), [[-1, 528]], OP.is_equal, 0.0, 3, 4)
    affine(f("FOLD"), f("ONE", 0, 544), [[0, 34], [1, 16]], OP.not_equal, 0.0, 0, 0)
    affine(f("RST"), f("RS0"), [[0, 2], [1, 17]], OP.not_equal, -BIG, 0, 0)
    iota(f("TA", 1734, 1784), [[0, 50]])
    iota(f("YC"), [[0, 19], [1, 17]])
    iota(f("SEG"), [[1, 8], [0, 19]], 1)
    iota(f("PRI"), [[0, 8], [-4096, 19]], 65536)
    iota(f("F0", 2048, W), [[0, 128]])
    affine(f("KEEP"), f("ONE", 0, 578), [[0, 34], [1, 17]], OP.not_equal, 0.0, 0, 0)
    iota(f("YT", 256, 512), [[0, 256]])
    for t in range(1, R):
        iota(f("F%d" % t, 2048, W), [[0, 128]])
    iota(f("OLI"), [[867, 2], [51, 16]], 56, small=False)
    iota(f("OLX"), [[0, 2], [1, 16]], small=False)
    for n in ("SPF", "SPS", "SPA", "SPX"):
        act(f(n), f("ONE", 0, 578), AF.Copy, 0.0)
    for n in ("D0F", "D0S", "D0X"):
        act(f(n, 0, 1776, 3), f("ONE"), AF.Copy, 0.0)
    for j in (1, 2):
        act(f("TD", j, 1734, 3), f("ONE", 0, 578), AF.Copy, 0.0)

    ts(f("PMI"), f("PI"), 15, OP.bitwise_and)
    cp(f("PM"), f("PMI"))
    pm = f("PM")
    ts(f("EE"), f("EI"), pm, OP.add)
    ts(f("EM"), f("EE"), 3856.0, OP.mult)
    ts(f("QD"), f("EM"), 16, OP.logical_shift_right)
    ts(f("H17"), f("QD"), 17.0, OP.is_ge, 17.0, OP.mult)
    ts(f("T1"), f("QD"), -17.0, OP.mult)
    ts(f("H256"), f("QD"), 17.0, OP.is_ge, 256.0, OP.mult)
    tt(f("XE"), f("QD"), f("H17"), OP.subtract)
    tt(f("YE"), f("T1"), f("EE"), OP.add)
    ts(f("OWN"), f("KI"), pm, OP.is_equal)
    for h in range(2):
        cp(f("L32", h, 32, 2), f("NDI", 16 * h, 16 * h + 16))
    ts(f("T1"), f("XE"), 0.0, OP.is_equal, 1000.0, OP.mult)
    ts(f("T3"), f("YE"), 0.0, OP.is_equal, 1000.0, OP.mult)
    cp(f("CM", ind=("L32", 0, 32)), f("OWN"))
    ts(f("T2"), f("XE"), 16.0, OP.mult, -17.0, OP.add)
    tt(f("T4"), f("XE"), f("T1"), OP.add)
    tt(f("T5"), f("T1"), f("T3"), OP.add)
    cp(f("UL"), f("ULI"))
    tt(f("T1"), f("T2"), f("YE"), OP.add)
    quant("UQ", "US", 0, 128, f("UT"))
    tt(f("T3"), f("H256"), f("T5"), OP.add)
    tt(f("T2"), f("T4"), f("YE"), OP.is_equal)
    cp(f("UQR", cast=dt.uint32), f("UQ", cast=dt.uint32, ind=("UL", 0, 8)))
    cp(f("USR"), f("US", ind=("UL", 0, 8)))
    for s in blocks:
        wait("v", s, 16)
    ts(f("NDF"), f("NDX"), 4.0, OP.mult)
    tt(f("T5"), f("T1"), f("T3"), OP.add)
    ts(f("T4"), f("T2"), 520.0, OP.mult)
    call("v", lambda e: e.transpose(T.N4[:, :], T.NDF[:, :]), [f("N4")], [f("NDF")])
    fill(f("SL", 0, 36, 18), 512)
    fill(f("SL", 17, 18), 512)
    fill(f("SL", 35, 36), 512)
    for h in range(2):
        ts(f("SL", 18 * h + 1, 18 * h + 17), f("N4", 16 * h, 16 * h + 16), 0.25, OP.mult)
    fill(f("PW", 512, 528), -BIG / 32)

    def scores(t, src):
        for a in range(2):
            quant("XQ%d" % t, "XS%d" % t, 256 * a, 256 * a + 256, f(src, 1024 * a, 1024 * a + 1024))
            mm(f("PS", 512 * a, 512 * a + 256), f("UQR"), f("USR"), f("XQ%d" % t, 256 * a, 256 * a + 256), f("XS%d" % t, 256 * a, 256 * a + 256))
        for a in range(2):
            tt(f("PW", 256 * a, 256 * a + 256), f("PS", 512 * a, 512 * a + 256), f("CM", 256 * a, 256 * a + 256), OP.mult)
        act(f("SG", 0, 272), f("PW", 0, 528, ind=("SL", 0, 17)))
        act(f("SG", 272, 544), f("PW", 0, 528, ind=("SL", 18, 35)))

    def unpack(t):
        for b in range(4):
            mm(f("PS", 1024 + 512 * b, 1536 + 512 * b), f("EQ", 128 * b, 128 * b + 128), f("ES", 128 * b, 128 * b + 128), f("XQ%d" % t), f("XS%d" % t))
        for b in range(4):
            act(f("F%d" % t, b, 2048, 4), f("PS", 1024 + 512 * b, 1536 + 512 * b))

    def differences(h):
        scan(f("DM", BLK * h + 1, BLK * h + 289), f("TA", SQ3 * h + 2, SQ3 * h + 864, 3), f("TA", SQ3 * h + 8, SQ3 * h + 870, 3), 0.0, OP.subtract, OP.subtract)

    scores(0, "XT")

    ts(f("T1"), f("T5"), 512.0, OP.min)
    ts(f("ARB", 0, 512), f("ARI"), -UNIT, OP.mult)
    fill(f("ARB", 512, 520), 0.0)
    tt(f("T3"), f("T1"), f("T4"), OP.max)
    fill(f("ARB", 520, 528), UNIT / 64)
    cp(f("NI"), f("N4"))
    cp(f("AL"), f("T3"))
    act(f("TA", 2, 1778, 3), f("ARB", ind=("AL", 0, 37)))
    fill(f("HL"), 0.0)
    for b in range(4):
        quant("EQ", "ES", 128 * b, 128 * b + 128, f("ET", 3 - b, 515 - b))
    unpack(0)
    ts(f("NHI"), f("NI"), 1920, OP.bitwise_and)
    ts(f("NLO"), f("NI"), 127, OP.bitwise_and)
    for h in range(2):
        fill(f("HL", 36 * h, 36 * h + 1), 2048.0)
        ts(f("HL", 36 * h + 18, 36 * h + 19), pm, 4.0, OP.mult, 64.0 * h, OP.add)
    for h in range(2):
        cp(f("HL", 36 * h + 1, 36 * h + 17), f("NHI", 16 * h, 16 * h + 16))
        cp(f("HL", 36 * h + 19, 36 * h + 35), f("NLO", 16 * h, 16 * h + 16))
    for h in range(2):
        fill(f("DM", BLK * h, BLK * h + 1), 0.0)
    for h in range(2):
        for j in range(2):
            tt(f("DM", BLK * h + 289 + 17 * j, BLK * h + 306 + 17 * j), f("HL", 36 * h + 18 * j, 36 * h + 18 * j + 17), f("HL", 36 * h + 18 * j + 1, 36 * h + 18 * j + 18), OP.subtract)

    def outer_list():
        tt(f("T2"), f("YE"), f("H17"), OP.add)
        cp(f("OUTL"), f("T2"))

    def bases():
        ts(f("CC"), f("SEG"), 1048576.0, OP.mult)
        for j in range(2):
            ts(f("ZK", 8 * j, 8 * j + 8), f("SEG", 0, 152, 19), 1048576.0, OP.mult, 71680.0, OP.add)

    def priorities():
        tt(f("CC"), f("CC"), f("PRI"), OP.add)
        fill(f("RK", 0, 1), -BIG)

    def member_columns(lo):
        for s in range(lo, lo + 4):
            a = 19 * s + 1
            tt(f("CC", a, a + 16), f("CC", a, a + 16), f("N4", 16 * (s % 2), 16 * (s % 2) + 16), OP.add)

    def output_list():
        ts(f("T1", 0, 1), pm, 3.0, OP.mult)
        ts(f("QD", 0, 32), f("OLX"), pm, OP.is_equal, 1736.0, OP.mult)
        ts(f("EM", 0, 32), f("OLI"), f("T1", 0, 1), OP.add)
        tt(f("EE", 0, 32), f("EM", 0, 32), f("QD", 0, 32), OP.max)
        cp(f("OL"), f("EE", 0, 32))

    def choose(s, j, slots):
        def slot():
            if slots:
                slots.pop(0)()
        for h in range(2):
            scan(f("RX", ROW * h, ROW * h + ROW), f("RST", 0, ROW), s(h), 0.0, OP.min, OP.max)
        slot()
        for h in range(2):
            ts(f("TT", ROW * h, ROW * h + ROW), f("RX", ROW * h, ROW * h + ROW), f("RX", ROW * h + 16, ROW * h + 17), OP.is_lt)
        slot()
        for h in range(2):
            total(f("IX", 2 * j + h, 2 * j + h + 1), f("TT", ROW * h, ROW * h + ROW))
        slot()
        for h in range(2):
            ts(f("KAP", BLK * h, BLK * h + BLK), f("YC"), f("IX", 2 * j + h, 2 * j + h + 1), OP.is_gt)
        for h in range(2):
            at = SEL * j + BLK * h
            scan(f("RS", at, at + BLK), f("KAP", BLK * h, BLK * h + BLK), f("DM", BLK * h, BLK * h + BLK), 0.0, OP.mult, OP.add)

    def key(j, io):
        a = 76 * io + 38 * j
        tt(f("KEY", a, a + 38), f("CC", a, a + 38), f("RS", SEL * j + 16, SEL * j + SEL, 17), OP.add if io else OP.subtract)

    def member_row(j, h):
        at = SEL * j + BLK * h
        return f("RS", at + 16, at + 289, 17)

    nxt = T.cores[(rank + 1) % len(T.cores)]
    rid, pid, _ = topo.addr(nxt)
    mask = sum(1 << e for e in topo.engines(core, nxt)[:8])
    engines = 8

    def send(t):
        q, s = f("SQ%d" % t, 0, 64, cast=dt.uint8), f("SS%d" % t, 0, 64)
        before("p", q[1] + s[1], [])
        g.remote_dma(T["LQ%d" % t][:, 0:64].bitcast(dt.uint8), q[0], T.sem["arr%d" % t], T.sem["left"], pid, rid, mask)
        g.remote_dma(T["LS%d" % t][:, 0:64], s[0], T.sem["arr%d" % t], T.sem["left"], pid, rid, mask)
        after("in%d" % t, [], [("LQ%d" % t, 0, 64, 1), ("LS%d" % t, 0, 64, 1)], "arr%d" % t, 2 * engines)
        count["arr%d" % t] = 2 * engines
        count["left"] = count.get("left", 0) + 2 * engines

    def clean(j):
        for h in range(2):
            act(f("CLN", 34 * j + ROW * h, 34 * j + ROW * h + ROW), member_row(j, h), AF.Identity, 1.0 / UNIT, 192.0)

    def scaled(j, out):
        act(out, f("CLN", 34 * j, 34 * j + 34), AF.Identity, UNIT, -192.0 * UNIT)

    def place_marks(j):
        for h in range(2):
            act(f("FG", 34 * j + ROW * h, 34 * j + ROW * h + ROW), f("YC", 0, ROW), AF.Abs, -1.0, f("IX", 2 * j + h, 2 * j + h + 1))

    def rows(sp, out, lo, h):
        scan(f(out, lo + SQ3 * h, SQ3 * h + SQ3, 3), f("KEEP", 0, 289), f(sp, 289 * h, 289 * h + 289), 0.0, OP.mult, OP.add)

    def columns(rv, d0):
        act(f(d0, 2, 1776, 3), f(rv, 0, 34, ind=("OUTL", 0, 37)), AF.Copy, -0.5 / UNIT)

    def column_signs(d0):
        act(f(d0, 1, 1776, 3), f(d0, 2, 1776, 3), AF.Sign)

    def steps(dst, d0, src, h):
        lo, hi = SQ3 * h, SQ3 * h + SQ3
        scan(f(dst, lo, hi), f(d0, lo, hi), f(src, lo, hi), 0.0, OP.mult, OP.add)

    for t in range(R):
        ft = "F%d" % t
        if t:
            scores(t, "F%d" % (t - 1))
            for h in range(2):
                steps("TA", "D0X", "TD", h)
            unpack(t)
        for h in range(2):
            scan(f("Z", 272 * h, 272 * h + 272), f("FOLD", 0, 272), f("SG", 272 * h, 272 * h + 272), 0.0, OP.mult, OP.add)
        choose(lambda h: f("Z", 272 * h + 15, 272 * h + 272, 16), 0, [lambda: differences(0), lambda: differences(1)] + ([outer_list] if t == 0 else []))
        for h in range(2):
            ts(f("GT", ROW * h, ROW * h + ROW), member_row(0, h), 0.0, OP.not_equal, -BIG, OP.mult)
        clean(0)
        scaled(0, f("RVF", 0, 34))
        scaled(0, f("SPF", 0, 578, 17))
        columns("RVF", "D0F")
        column_signs("D0F")
        if t == 0:
            bases()
        for h in range(2):
            tt(f("S2", ROW * h, ROW * h + ROW), f("Z", 272 * h + 15, 272 * h + 272, 16), f("GT", ROW * h, ROW * h + ROW), OP.add)
        if t == 0:
            choose(lambda h: f("S2", ROW * h, ROW * h + ROW), 1, [priorities, lambda: member_columns(0), lambda: member_columns(4)])
            key(0, 0)
            key(0, 1)
        else:
            choose(lambda h: f("S2", ROW * h, ROW * h + ROW), 1, [lambda: key(0, 0), lambda: key(0, 1)])
        rows("SPF", "TA", 0, 0)
        tt(f("KC"), f("RS", 305, 2 * SEL, BLK), f("RS", 322, 2 * SEL, BLK), OP.add)
        key(1, 0)
        key(1, 1)
        for b in range(4):
            ts(f("KL", 4 * b, 4 * b + 4), f("KC"), float(b), OP.add)
        act(f("KF"), f(ft, ind=("KL", 0, 16)))
        for io in range(2):
            scan(f("RK", 76 * io + 1, 76 * io + 77), f("KEY", 76 * io, 76 * io + 76), f("KEY", 76 * io, 76 * io + 76), -BIG, OP.max, OP.max)
        scan(f("RK", 153, 229), f("KEY", 0, 76), f("RK", 0, 76), -BIG, OP.max, OP.min)
        tt(f("DEC", 0, 8), f("RK", 19, 153, 19), f("ZK", 0, 8), OP.max)
        scan(f("RK", 229, 305), f("KEY", 76, 152), f("RK", 76, 152), -BIG, OP.max, OP.min)
        ts(f("DCM", 0, 8), f("DEC", 0, 8), 4095, OP.bitwise_and)
        tt(f("DEC", 8, 16), f("RK", 171, 305, 19), f("ZK", 8, 16), OP.max)
        for b in range(4):
            ts(f("LL", 8 * b, 8 * b + 8), f("DCM", 0, 8), float(b), OP.add)
            act(f("AB", 128 * b, 128 * b + 128), f(ft, ind=("LL", 8 * b, 8 * b + 8)))
            if b == 1:
                ts(f("DCM", 8, 16), f("DEC", 8, 16), 4095, OP.bitwise_and)
        for b in range(4):
            ts(f("LL", 32 + 8 * b, 40 + 8 * b), f("DCM", 8, 16), float(b), OP.add)
        rows("SPF", "TA", 0, 1)
        clean(1)
        place_marks(0)
        scaled(1, f("RVS", 0, 34))
        scaled(1, f("SPS", 0, 578, 17))
        place_marks(1)
        act(f("SPA", 0, 578, 17), f("RVS", 0, 34), AF.Abs)
        act(f("TA", 1, 1734, 3), f("TA", 0, 1734, 3), AF.Abs)
        act(f("FS"), f("FG"), AF.Sign)
        columns("RVS", "D0S")
        column_signs("D0S")
        for b in range(4):
            tt(f("IO2", 128 * b, 128 * b + 128), f(ft, ind=("LL", 32 + 8 * b, 40 + 8 * b)), f("AB", 128 * b, 128 * b + 128), OP.add)

        def larger(b):
            tt(f("M2", 64 * b, 64 * b + 64), f("IO2", 128 * b, 128 * b + 64), f("IO2", 128 * b + 64, 128 * b + 128), OP.max)

        def half(a):
            ts(f("MH", 128 * a, 128 * a + 128), f("M2", 128 * a, 128 * a + 128), 0.5, OP.mult)

        def less(b):
            tt(f("YT", b, 256, 4), f("MH", 64 * b, 64 * b + 64), f("KF", 64 * b, 64 * b + 64), OP.subtract)

        for fn, b in ((larger, 0), (larger, 1), (larger, 2), (half, 0), (larger, 3), (less, 0), (half, 1), (less, 1), (less, 2), (less, 3)):
            fn(b)
        quant("SQ%d" % t, "SS%d" % t, 0, 128, f("YT"))
        send(t)
        if t == 0:
            for i in range(R):
                dma("y", f("LQ%d" % i, 64, 128, cast=dt.uint8), f("SQ0", 64, 128, cast=dt.uint8))
                dma("y", f("LS%d" % i, 64, 128), f("SS0", 64, 128))
        for h in range(2):
            steps("TB", "D0F", "TA", h)
        tt(f("FH"), f("FS", 0, 34), f("FS", 34, 68), OP.add)
        act(f("FV", 0, 34), f("FH"), AF.Identity, 2.0, -3.0)
        act(f("SPX", 0, 578, 17), f("FH"), AF.Identity, 2.0, -3.0)
        act(f("D0X", 1, 1776, 3), f("FV", 0, 34, ind=("OUTL", 0, 37)))
        act(f("YW"), f("YT", 0, 256), AF.Copy, 32.0)
        for h in range(2):
            rows("SPS", "TB", 0, h)
        for h in range(2):
            rows("SPA", "TB", 1, h)
        for h in range(2):
            steps("TC", "D0S", "TB", h)
        rows("SPX", "D0X", 2, 0)
        for h in range(2):
            ts(f("TD", SQ3 * h, SQ3 * h + SQ3, 3), f("TC", SQ3 * h + 2, SQ3 * h + SQ3, 3), 3.0 * UNIT, OP.min, -3.0 * UNIT, OP.max)
        if t == 1:
            output_list()
        if t == R - 1:
            rows("SPX", "D0X", 2, 1)
            quant("VQ", "VS", 0, 128, f("VT"))
            for h in range(2):
                steps("TA", "D0X", "TD", h)
            act(f("OAO"), f("TA", ind=("OL", 0, 32)), AF.Copy, -1.0 / UNIT)
            dma("y", (T.oa[:, :], []), f("OAO"))
        for b in range(4):
            mm(f("PS", 1024 + 512 * b, 1152 + 512 * b), f("WQ", 128 * b, 128 * b + 128), f("WS", 128 * b, 128 * b + 128), f("LQ%d" % t), f("LS%d" % t))
        for b in range(4):
            tt(f("V32", 64 * b, 64 * b + 64), f("PS", 1024 + 512 * b, 1088 + 512 * b), f("YW", b, 256, 4), OP.add)
        ts(f("VV"), f("V32"), 0.03125, OP.mult)
        if t < R - 1:
            rows("SPX", "D0X", 2, 1)
        cp(f(ft, ind=("KL", 0, 16)), f("VV"))

    for a in range(2):
        lo, hi = 256 * a, 256 * a + 256
        quant("XQ3", "XS3", lo, hi, f("F2", 1024 * a, 1024 * a + 1024))
        mm(f("PS", 512 * a, 512 * a + 256), f("VQ"), f("VS"), f("XQ3", lo, hi), f("XS3", lo, hi))
        dma("y", (T.oc[:, 4 * lo:4 * hi], []), f("XQ3", lo, hi, cast=dt.uint8))
    act(f("YO", 0, 256), f("PS", 0, 256))
    dma("s", (T.y[:, 0:256], []), f("YO", 0, 256))
    cp(f("YO", 256, 512), f("PS", 512, 768))
    dma("y", (T.y[:, 256:512], []), f("YO", 256, 512))
    for k in range(4):
        dma("s" if k % 2 else "y", (T.osc[4 * k:4 * k + 4, :], []), (T.XS3[32 * k:32 * k + 4, 0:512], [("XS3", 0, 512, 1)]))
    for sem in count:
        if sem != "dma":
            wait("p", sem, count[sem])
